import numpy as np
import ml_dtypes


def mxq(x, axis, fmt="e4m3"):
    dtype, down = {"e4m3": (ml_dtypes.float8_e4m3fn, 7), "e5m2": (ml_dtypes.float8_e5m2, 14)}[fmt]
    v = np.moveaxis(np.asarray(x, np.float32).astype(ml_dtypes.bfloat16).astype(np.float64), axis, -1)
    blocks = v.reshape(v.shape[:-1] + (-1, 32))
    amax = np.abs(blocks).max(-1, keepdims=True)
    byte = np.maximum(np.where(amax > 0, np.frexp(amax)[1] - 1 + 127, 0) - down, 1)
    scale = np.exp2(byte - 127.0)
    codes = (blocks / scale).astype(np.float32).astype(dtype).astype(np.float64)
    return np.moveaxis((codes * scale).reshape(v.shape), -1, axis)


WIDE = False


def mx_kscale(k):
    if not WIDE:
        return np.ones(k)
    levels = np.array([10, -10, 5, -5, 0])
    if k % 512:
        return np.exp2(np.random.permutation(np.resize(levels, k // 32))).repeat(32)
    a = np.empty((k // 512, 16))
    for p in range(k // 512):
        a[p, :8] = np.random.permutation(np.resize(levels, 8))
        for g in range(8):
            far = levels[np.abs(levels - a[p, g]) >= 10]
            a[p, g + 8] = far[np.random.randint(len(far))]
    return np.exp2(a.ravel()).repeat(32)


def f64(x):
    return np.asarray(x).astype(np.float64)


def striped(idx):
    return np.tile(idx.reshape(-1, 16).T, (8, 1)).astype(np.uint16)


def unstriped(offs):
    return offs[:16].T.reshape(-1).astype(np.int64)


E2M1 = np.array([0.0, 0.5, 1.0, 1.5, 2.0, 3.0, 4.0, 6.0, -0.0, -0.5, -1.0, -1.5, -2.0, -3.0, -4.0, -6.0])


def pack_weight(w, fmt):
    k, n = w.shape
    w = f64(np.asarray(w, np.float32).astype(ml_dtypes.bfloat16)).reshape(k // 32, 32, n)
    amax = np.abs(w).max(1)
    if fmt == "e4m3":
        byte = np.frexp(amax)[1] - 1 + 127 - 7
    else:
        mant, ex = np.frexp(amax / 6.0)
        byte = np.where(mant > 0.5, ex, ex - 1) + 127
    byte = np.clip(np.where(amax > 0, byte, 1), 1, 254)
    scaled = (w * np.exp2(127.0 - byte)[:, None, :]).reshape(k, n).astype(np.float32)
    by_word = np.ascontiguousarray(scaled.reshape(k // 512, 128, 4, n).transpose(0, 1, 3, 2))
    if fmt == "e4m3":
        words = by_word.astype(ml_dtypes.float8_e4m3fn).view(np.uint8)
    else:
        c = by_word.astype(ml_dtypes.float4_e2m1fn).view(np.uint8) & 0xF
        words = (c[..., 0::2] | (c[..., 1::2] << 4)).reshape(k // 512, 128, 2 * n)
    return np.ascontiguousarray(words), np.ascontiguousarray(byte.astype(np.uint8).reshape(k // 512, 16, n))


def unpack_weight(words, scales, fmt):
    g, _, n = scales.shape
    words = np.ascontiguousarray(words).reshape(g, 128, n, -1)
    if fmt == "e4m3":
        vals = words.view(ml_dtypes.float8_e4m3fn).astype(np.float64)
    else:
        nib = np.empty((g, 128, n, 4), np.uint8)
        nib[..., 0::2] = words & 0xF
        nib[..., 1::2] = words >> 4
        vals = E2M1[nib]
    vals = vals * np.repeat(np.exp2(scales.astype(np.float64) - 127.0), 8, axis=1)[..., None]
    return vals.transpose(0, 1, 3, 2).reshape(g * 512, n)


def gelu(v):
    return 0.5 * v * (1.0 + np.tanh(np.sqrt(2.0 / np.pi) * (v + 0.044715 * v**3)))


K, H, N, T, S, T2 = 512, 1024, 384, 4096, 1024, 2048

def setup_inputs():
    n = np.random.standard_normal
    s = mx_kscale(K)[:, None]
    u = mx_kscale(H)[:, None]
    tab_words, tab_scales = pack_weight(n((K, T)) * s, "e4m3")
    w1 = (n((K, H)) / np.sqrt(K) / s * u.T).astype(np.float32)
    w2_words, w2_scales = pack_weight(n((K, H)) / np.sqrt(K) / s * u.T, "e2m1")
    b1 = (0.5 * n(H) * u[:, 0]).astype(np.float32)
    b2 = (0.5 * n(H) * u[:, 0]).astype(np.float32)
    w3 = (n((H, N)) / np.sqrt(H) / u).astype(np.float32)
    b3 = (0.5 * n(N)).astype(np.float32)
    wgo = np.exp(0.3 * n((128, S))).astype(np.float32)
    offs = striped(np.random.permutation(T)[:S])
    offs2 = striped(np.random.permutation(T2)[:S])
    return dict(tab_words=tab_words, tab_scales=tab_scales, offs=offs, w1=w1, b1=b1, w2_words=w2_words,
                w2_scales=w2_scales, b2=b2, w3=w3, b3=b3, wgo=wgo, offs2=offs2)

def reference(tab_words, tab_scales, offs, w1, b1, w2_words, w2_scales, b2, w3, b3, wgo, offs2):
    v = unpack_weight(tab_words, tab_scales, "e4m3")[:, unstriped(offs)]
    w2 = unpack_weight(w2_words, w2_scales, "e2m1")
    a = (mxq(f64(w1), 0, "e4m3").T @ v) + f64(b1)[:, None]
    b = (w2.T @ v) + f64(b2)[:, None]
    h = np.maximum(a, b)
    y = (mxq(f64(w3), 0, "e4m3").T @ mxq(h, 0, "e4m3")) + f64(b3)[:, None]
    out = np.zeros((N, T2))
    out[:, unstriped(offs2)] = np.tile(f64(wgo), (N // 128, 1)) * y
    return out

@@ -1,0 +1,262 @@
+from contextlib import ExitStack
+
+import concourse.mybir as mybir
+
+K, H, N, T, S, T2 = 512, 1024, 384, 4096, 1024, 2048
+FLOPS = 2 * (2 * K * H * S + H * N * S)
+
+F32 = mybir.dt.float32
+BF16 = mybir.dt.bfloat16
+I32 = mybir.dt.int32
+U32 = mybir.dt.uint32
+U16 = mybir.dt.uint16
+U8 = mybir.dt.uint8
+FP8X4 = mybir.dt.float8_e4m3fn_x4
+FP4X4 = mybir.dt.float4_e2m1fn_x4
+ADD = mybir.AluOpType.add
+MAX = mybir.AluOpType.max
+MULT = mybir.AluOpType.mult
+IDENTITY = mybir.ActivationFunctionType.Identity
+
+P = 128
+PACK = 4
+PASS = P * PACK
+CHUNK = 512
+PASSES = H // PASS
+CHUNKS = S // CHUNK
+BLOCKS = N // P
+LIST_COLS = CHUNK // 16
+
+
+def tile_list_maxout_point_features_kernel(
+    tc, tab_words, tab_scales, offs, w1, b1, w2_words, w2_scales, b2, w3, b3, wgo, offs2, out
+):
+    nc = tc.nc
+    with ExitStack() as ctx:
+        lists = ctx.enter_context(tc.tile_pool(name="lists", bufs=1))
+        keep = ctx.enter_context(tc.tile_pool(name="keep", bufs=1))
+        work = ctx.enter_context(tc.tile_pool(name="work", bufs=2))
+        psum = ctx.enter_context(tc.psum_pool(name="psum", bufs=1))
+
+        picks = lists.tile([P, S // 16], U16, name="picks")
+        places = lists.tile([P, S // 16], U16, name="places")
+        nc.sync.dma_start(picks[:], offs)
+        nc.sync.dma_start(places[:], offs2)
+
+        table = keep.tile([P, T], I32, name="table", tag="e", align_bytes=64)
+        table_scales = keep.tile([P, T], U8, name="table_scales", tag="c", align_bytes=64)
+        w2_raw = keep.tile([P, 2 * H], U8, name="w2_raw", tag="a", align_bytes=64)
+        w2_scales_raw = keep.tile([P, H], U8, name="w2_scales_raw", tag="b", align_bytes=64)
+        bias1 = keep.tile([P, PASSES, PACK], F32, name="bias1")
+        bias2 = keep.tile([P, PASSES, PACK], F32, name="bias2")
+        bias3 = keep.tile([P, BLOCKS], F32, name="bias3")
+
+        nc.vector.memset(table_scales[:].bitcast(I32), 0)
+        nc.vector.memset(w2_scales_raw[:].bitcast(I32), 0)
+        nc.scalar.dma_start(bias2[:], b2.rearrange("(g p t) -> p g t", p=P, t=PACK))
+        nc.scalar.dma_start(bias1[:], b1.rearrange("(g p t) -> p g t", p=P, t=PACK))
+        with nc.allow_non_contiguous_dma(reason="one bias value a partition"):
+            nc.scalar.dma_start(bias3[:], b3.rearrange("(c p) -> p c", p=P))
+        nc.scalar.dma_start(table_scales[0:P:8, :].bitcast(I32), tab_scales[0].bitcast(I32))
+        for q in range(4):
+            nc.scalar.dma_start(
+                w2_scales_raw[32 * q : 32 * q + 4, :].bitcast(I32), w2_scales[0, 4 * q : 4 * q + 4, :].bitcast(I32)
+            )
+        nc.sync.dma_start(w2_raw[:].bitcast(I32), w2_words[0].bitcast(I32))
+        nc.sync.dma_start(table[:], tab_words[0].rearrange("p t i -> p (t i)").bitcast(I32))
+
+        def chunk_list(tile, c):
+            return tile[:, c * LIST_COLS : (c + 1) * LIST_COLS]
+
+        def chunk_cols(c):
+            return slice(c * CHUNK, (c + 1) * CHUNK)
+
+        w2_codes = keep.tile([P, 2 * H], U8, name="w2_codes", align_bytes=64)
+        w2_planes = keep.tile([P, H], U8, name="w2_planes", align_bytes=64)
+        picked_scales = keep.tile([P, S], U8, name="picked_scales", tag="d", align_bytes=64)
+        v_planes = keep.tile([P, S], U8, name="v_planes", align_bytes=64)
+        nc.vector.memset(v_planes[:].bitcast(I32), 0)
+
+        nc.vector.tensor_copy(
+            w2_codes[:].bitcast(U16).rearrange("p (g t m) -> p g t m", g=PASSES, t=PACK),
+            w2_raw[:].bitcast(U16).rearrange("p (g m t) -> p g t m", g=PASSES, t=PACK),
+        )
+        nc.vector.tensor_copy(picked_scales[:], table_scales[:].indirect(picks[:]))
+        nc.vector.tensor_copy(
+            w2_planes[:].rearrange("p (g t m) -> p g t m", g=PASSES, t=PACK),
+            w2_scales_raw[:].rearrange("p (g m t) -> p g t m", g=PASSES, t=PACK),
+        )
+        w1_rows = w1.rearrange("(p j) r -> p j r", j=PACK)
+        w1_raw = []
+        for g in range(PASSES):
+            raw = keep.tile([P, PACK, PASS], F32, name="w1_raw", tag="ab"[g], align_bytes=64)
+            nc.sync.dma_start(raw[:], w1_rows[:, :, g * PASS : (g + 1) * PASS])
+            w1_raw.append(raw)
+        for q in range(4):
+            nc.scalar.dma_start(
+                v_planes[32 * q : 32 * q + 4, :].bitcast(I32), picked_scales[32 * q : 32 * q + 32 : 8, :].bitcast(I32)
+            )
+        v_all = keep.tile([P, S], U32, name="v_all", tag="c", align_bytes=64)
+        for c in range(CHUNKS):
+            nc.vector.tensor_copy(v_all[:, chunk_cols(c)], table[:].bitcast(U32).indirect(chunk_list(picks, c)))
+        v_codes = [v_all[:, chunk_cols(c)] for c in range(CHUNKS)]
+        v_scales = [v_planes[:, chunk_cols(c)] for c in range(CHUNKS)]
+
+        w1_codes, w1_planes = [], []
+        w3_codes, w3_planes = [], []
+        for g in range(PASSES):
+            w1_codes.append(keep.tile([P, PASS], U32, name="w1_codes%d" % g, align_bytes=64))
+            w1_planes.append(keep.tile([P, PASS], U8, name="w1_planes%d" % g, align_bytes=64))
+            w3_codes.append(keep.tile([P, N], U32, name="w3_codes%d" % g, align_bytes=64))
+            w3_planes.append(keep.tile([P, N], U8, name="w3_planes%d" % g, align_bytes=64))
+
+        def round_w1(g, copy):
+            grouped = keep.tile([P, PACK * PASS], BF16, name="w1_grouped", tag="e", align_bytes=64)
+            copy(
+                grouped[:].rearrange("p (t m j) -> p m j t", t=PACK, j=PACK),
+                w1_raw[g][:].rearrange("p j (m t) -> p m j t", t=PACK),
+            )
+            return grouped
+
+        def quantize_w1(g, grouped):
+            nc.vector.quantize_mx(w1_codes[g][:].bitcast(FP8X4), w1_planes[g][:], grouped[:])
+
+        def load_w3(g):
+            raw = keep.tile([P, PACK, N], F32, name="w3_raw", tag="da"[g], align_bytes=64)
+            nc.sync.dma_start(raw[:], w3[g * PASS : (g + 1) * PASS, :].rearrange("(p j) n -> p j n", j=PACK))
+            return raw
+
+        def round_w3(raw, copy):
+            grouped = work.tile([P, PACK * N], BF16, name="w3_grouped", align_bytes=64)
+            copy(
+                grouped[:].rearrange("p (c i j) -> p c j i", i=4, j=PACK),
+                raw[:].rearrange("p j (c i) -> p c j i", i=4),
+            )
+            return grouped
+
+        def quantize_w3(g, grouped):
+            for lo, hi in ((0, 256), (256, N)):
+                nc.vector.quantize_mx(
+                    w3_codes[g][:, lo:hi].bitcast(FP8X4), w3_planes[g][:, lo:hi], grouped[:, PACK * lo : PACK * hi]
+                )
+
+        second = {}
+
+        def second_pieces(c, g):
+            for t in range(PACK):
+                cols = g * PASS + t * P
+                bank = psum.tile([P, CHUNK], F32, name="bank_b", tag="bank_b", bufs=2)
+                nc.tensor.matmul_mx(
+                    bank[:],
+                    lhsT=w2_codes[:, 2 * cols : 2 * (cols + P)].bitcast(FP4X4),
+                    lhsT_scale=w2_planes[:, cols : cols + P],
+                    rhs=v_codes[c].bitcast(FP8X4),
+                    rhs_scale=v_scales[c],
+                    start=True,
+                    stop=True,
+                )
+                piece = keep.tile([P, CHUNK], F32, name="piece", tag="piece%d%d" % (g, t), align_bytes=64)
+                nc.scalar.activation(piece[:], bank[:], IDENTITY, bias=bias2[:, g, t : t + 1])
+                second[c, g, t] = piece
+
+        def maxout(c, g):
+            units = keep.tile([P, PACK, CHUNK], BF16, name="units", tag="units%d" % g, align_bytes=64)
+            for t in range(PACK):
+                bank = psum.tile([P, CHUNK], F32, name="bank_a", tag="bank_a", bufs=3)
+                nc.tensor.matmul_mx(
+                    bank[:],
+                    lhsT=w1_codes[g][:, t * P : (t + 1) * P].bitcast(FP8X4),
+                    lhsT_scale=w1_planes[g][:, t * P : (t + 1) * P],
+                    rhs=v_codes[c].bitcast(FP8X4),
+                    rhs_scale=v_scales[c],
+                    start=True,
+                    stop=True,
+                )
+                nc.vector.scalar_tensor_tensor(
+                    units[:, t, :], bank[:], bias1[:, g, t : t + 1], second[c, g, t][:], ADD, MAX
+                )
+            return units
+
+        def interleave(units, copy):
+            grouped = work.tile([P, PACK * CHUNK], BF16, name="h_grouped", align_bytes=64)
+            copy(
+                grouped[:].rearrange("p (c i t) -> p c t i", i=4, t=PACK),
+                units[:].rearrange("p t (c i) -> p c t i", i=4),
+            )
+            return grouped
+
+        def quantize_h(grouped):
+            codes = work.tile([P, CHUNK], U32, name="h_codes", align_bytes=64, bufs=4)
+            planes = work.tile([P, CHUNK], U8, name="h_planes", align_bytes=64, bufs=4)
+            nc.vector.quantize_mx(codes[:].bitcast(FP8X4), planes[:], grouped[:])
+            return codes, planes
+
+        def output_map(h):
+            banks = []
+            for b in range(BLOCKS):
+                bank = psum.tile([P, CHUNK], F32, name="bank_y", tag="bank_y", bufs=3)
+                for g in range(PASSES):
+                    nc.tensor.matmul_mx(
+                        bank[:],
+                        lhsT=w3_codes[g][:, b * P : (b + 1) * P].bitcast(FP8X4),
+                        lhsT_scale=w3_planes[g][:, b * P : (b + 1) * P],
+                        rhs=h[g][0][:].bitcast(FP8X4),
+                        rhs_scale=h[g][1][:],
+                        start=(g == 0),
+                        stop=(g == PASSES - 1),
+                    )
+                banks.append(bank)
+            return banks
+
+        def add_bias3(bank, b, tag):
+            y = keep.tile([P, CHUNK], F32, name="y", tag=tag, align_bytes=64)
+            nc.scalar.activation(y[:], bank[:], IDENTITY, bias=bias3[:, b : b + 1])
+            return y
+
+        pages = [keep.tile([P, T2], F32, name="page%d" % b) for b in range(BLOCKS)]
+
+        def scatter(c, b, y):
+            nc.vector.tensor_tensor(
+                pages[b][:].indirect(chunk_list(places, c)), y[:], weights[:, c * CHUNK : (c + 1) * CHUNK], MULT
+            )
+
+        w3_raw0 = load_w3(0)
+        second_pieces(0, 0)
+        quantize_w1(0, round_w1(0, nc.vector.tensor_copy))
+        w3_raw1 = load_w3(1)
+        w1_grouped1 = round_w1(1, nc.scalar.copy)
+        weights = keep.tile([P, S], F32, name="weights", tag="b", align_bytes=64)
+        nc.sync.dma_start(weights[:], wgo)
+        units00 = maxout(0, 0)
+        second_pieces(0, 1)
+        quantize_w1(1, w1_grouped1)
+        w3_grouped0 = round_w3(w3_raw0, nc.scalar.copy)
+        grouped00 = interleave(units00, nc.scalar.copy)
+        units01 = maxout(0, 1)
+        w3_grouped1 = round_w3(w3_raw1, nc.vector.tensor_copy)
+        grouped01 = interleave(units01, nc.vector.tensor_copy)
+        quantize_w3(0, w3_grouped0)
+        quantize_w3(1, w3_grouped1)
+        h01 = quantize_h(grouped01)
+        h00 = quantize_h(grouped00)
+        for page in pages:
+            nc.vector.memset(page[:], 0.0)
+        second_pieces(1, 0)
+        banks0 = output_map((h00, h01))
+        y00 = add_bias3(banks0[0], 0, "y00")
+        units10 = maxout(1, 0)
+        second_pieces(1, 1)
+        scatter(0, 0, y00)
+        grouped10 = interleave(units10, nc.scalar.copy)
+        units11 = maxout(1, 1)
+        y01 = add_bias3(banks0[1], 1, "piece11")
+        grouped11 = interleave(units11, nc.scalar.copy)
+        scatter(0, 1, y01)
+        h10 = quantize_h(grouped10)
+        h11 = quantize_h(grouped11)
+        y02 = add_bias3(banks0[2], 2, "units1")
+        banks1 = output_map((h10, h11))
+        scatter(0, 2, y02)
+        for b in range(BLOCKS):
+            scatter(1, b, add_bias3(banks1[b], b, "y1%d" % b))
+            nc.sync.dma_start(out[b * P : (b + 1) * P, :], pages[b][:])

@@ -36,6 +36,7 @@ def tile_list_maxout_point_features_kernel(
         lists = ctx.enter_context(tc.tile_pool(name="lists", bufs=1))
         keep = ctx.enter_context(tc.tile_pool(name="keep", bufs=1))
         work = ctx.enter_context(tc.tile_pool(name="work", bufs=2))
+        late = ctx.enter_context(tc.tile_pool(name="late", bufs=1))
         psum = ctx.enter_context(tc.psum_pool(name="psum", bufs=1))
 
         picks = lists.tile([P, S // 16], U16, name="picks")
@@ -53,10 +54,10 @@ def tile_list_maxout_point_features_kernel(
 
         nc.vector.memset(table_scales[:].bitcast(I32), 0)
         nc.vector.memset(w2_scales_raw[:].bitcast(I32), 0)
-        nc.scalar.dma_start(bias2[:], b2.rearrange("(g p t) -> p g t", p=P, t=PACK))
-        nc.scalar.dma_start(bias1[:], b1.rearrange("(g p t) -> p g t", p=P, t=PACK))
+        nc.sync.dma_start(bias2[:], b2.rearrange("(g p t) -> p g t", p=P, t=PACK))
+        nc.sync.dma_start(bias1[:], b1.rearrange("(g p t) -> p g t", p=P, t=PACK))
         with nc.allow_non_contiguous_dma(reason="one bias value a partition"):
-            nc.scalar.dma_start(bias3[:], b3.rearrange("(c p) -> p c", p=P))
+            nc.sync.dma_start(bias3[:], b3.rearrange("(c p) -> p c", p=P))
         nc.scalar.dma_start(table_scales[0:P:8, :].bitcast(I32), tab_scales[0].bitcast(I32))
         for q in range(4):
             nc.scalar.dma_start(
@@ -177,8 +178,9 @@ def tile_list_maxout_point_features_kernel(
                 )
             return units
 
-        def interleave(units, copy):
-            grouped = work.tile([P, PACK * CHUNK], BF16, name="h_grouped", align_bytes=64)
+        def interleave(units, copy, grouped=None):
+            if grouped is None:
+                grouped = work.tile([P, PACK * CHUNK], BF16, name="h_grouped", align_bytes=64)
             copy(
                 grouped[:].rearrange("p (c i t) -> p c t i", i=4, t=PACK),
                 units[:].rearrange("p t (c i) -> p c t i", i=4),
@@ -213,7 +215,7 @@ def tile_list_maxout_point_features_kernel(
             nc.scalar.activation(y[:], bank[:], IDENTITY, bias=bias3[:, b : b + 1])
             return y
 
-        pages = [keep.tile([P, T2], F32, name="page%d" % b) for b in range(BLOCKS)]
+        pages = []
 
         def scatter(c, b, y):
             nc.vector.tensor_tensor(
@@ -230,8 +232,11 @@ def tile_list_maxout_point_features_kernel(
         units00 = maxout(0, 0)
         second_pieces(0, 1)
         quantize_w1(1, w1_grouped1)
+        pages.append(keep.tile([P, T2], F32, name="page0", tag="e", align_bytes=64))
+        nc.gpsimd.memset(pages[0][:], 0.0)
         w3_grouped0 = round_w3(w3_raw0, nc.scalar.copy)
-        grouped00 = interleave(units00, nc.scalar.copy)
+        grouped00 = late.tile([P, PACK * CHUNK], BF16, name="grouped00", align_bytes=64, offset=6144)
+        interleave(units00, nc.scalar.copy, grouped00)
         units01 = maxout(0, 1)
         w3_grouped1 = round_w3(w3_raw1, nc.vector.tensor_copy)
         grouped01 = interleave(units01, nc.vector.tensor_copy)
@@ -239,8 +244,9 @@ def tile_list_maxout_point_features_kernel(
         quantize_w3(1, w3_grouped1)
         h01 = quantize_h(grouped01)
         h00 = quantize_h(grouped00)
-        for page in pages:
-            nc.vector.memset(page[:], 0.0)
+        for b in (1, 2):
+            pages.append(late.tile([P, T2], F32, name="page%d" % b, align_bytes=64, offset=(b - 1) * 8192))
+            nc.gpsimd.memset(pages[b][:], 0.0)
         second_pieces(1, 0)
         banks0 = output_map((h00, h01))
         y00 = add_bias3(banks0[0], 0, "y00")

@@ -35,36 +35,9 @@ def tile_list_maxout_point_features_kernel(
     with ExitStack() as ctx:
         lists = ctx.enter_context(tc.tile_pool(name="lists", bufs=1))
         keep = ctx.enter_context(tc.tile_pool(name="keep", bufs=1))
-        work = ctx.enter_context(tc.tile_pool(name="work", bufs=2))
         late = ctx.enter_context(tc.tile_pool(name="late", bufs=1))
+        tail = ctx.enter_context(tc.tile_pool(name="tail", bufs=1))
         psum = ctx.enter_context(tc.psum_pool(name="psum", bufs=1))
-
-        picks = lists.tile([P, S // 16], U16, name="picks")
-        places = lists.tile([P, S // 16], U16, name="places")
-        nc.sync.dma_start(picks[:], offs)
-        nc.sync.dma_start(places[:], offs2)
-
-        table = keep.tile([P, T], I32, name="table", tag="e", align_bytes=64)
-        table_scales = keep.tile([P, T], U8, name="table_scales", tag="c", align_bytes=64)
-        w2_raw = keep.tile([P, 2 * H], U8, name="w2_raw", tag="a", align_bytes=64)
-        w2_scales_raw = keep.tile([P, H], U8, name="w2_scales_raw", tag="b", align_bytes=64)
-        bias1 = keep.tile([P, PASSES, PACK], F32, name="bias1")
-        bias2 = keep.tile([P, PASSES, PACK], F32, name="bias2")
-        bias3 = keep.tile([P, BLOCKS], F32, name="bias3")
-
-        nc.vector.memset(table_scales[:].bitcast(I32), 0)
-        nc.vector.memset(w2_scales_raw[:].bitcast(I32), 0)
-        nc.sync.dma_start(bias2[:], b2.rearrange("(g p t) -> p g t", p=P, t=PACK))
-        nc.sync.dma_start(bias1[:], b1.rearrange("(g p t) -> p g t", p=P, t=PACK))
-        with nc.allow_non_contiguous_dma(reason="one bias value a partition"):
-            nc.sync.dma_start(bias3[:], b3.rearrange("(c p) -> p c", p=P))
-        nc.scalar.dma_start(table_scales[0:P:8, :].bitcast(I32), tab_scales[0].bitcast(I32))
-        for q in range(4):
-            nc.scalar.dma_start(
-                w2_scales_raw[32 * q : 32 * q + 4, :].bitcast(I32), w2_scales[0, 4 * q : 4 * q + 4, :].bitcast(I32)
-            )
-        nc.sync.dma_start(w2_raw[:].bitcast(I32), w2_words[0].bitcast(I32))
-        nc.sync.dma_start(table[:], tab_words[0].rearrange("p t i -> p (t i)").bitcast(I32))
 
         def chunk_list(tile, c):
             return tile[:, c * LIST_COLS : (c + 1) * LIST_COLS]
@@ -72,36 +45,71 @@ def tile_list_maxout_point_features_kernel(
         def chunk_cols(c):
             return slice(c * CHUNK, (c + 1) * CHUNK)
 
-        w2_codes = keep.tile([P, 2 * H], U8, name="w2_codes", align_bytes=64)
-        w2_planes = keep.tile([P, H], U8, name="w2_planes", align_bytes=64)
-        picked_scales = keep.tile([P, S], U8, name="picked_scales", tag="d", align_bytes=64)
-        v_planes = keep.tile([P, S], U8, name="v_planes", align_bytes=64)
-        nc.vector.memset(v_planes[:].bitcast(I32), 0)
+        picks = lists.tile([P, S // 16], U16, name="picks")
+        places = lists.tile([P, S // 16], U16, name="places")
+        table = keep.tile([P, T], I32, name="table", tag="table", align_bytes=64)
+        table_scales = keep.tile([P, T], U8, name="table_scales", tag="table_scales", align_bytes=64)
+        w2_raw = keep.tile([P, 2 * H], U8, name="w2_raw", align_bytes=64)
+        w2_scales_raw = keep.tile([P, H], U8, name="w2_scales_raw", align_bytes=64)
+        planes = keep.tile([P, S + H], U8, name="planes", align_bytes=64)
+        bias1 = keep.tile([P, PASSES, PACK], F32, name="bias1")
+        bias2 = keep.tile([P, PASSES, PACK], F32, name="bias2")
+        bias3 = keep.tile([P, BLOCKS], F32, name="bias3")
+        pages = [keep.tile([P, T2], F32, name="page%d" % b, align_bytes=64) for b in range(1)]
 
+        nc.gpsimd.memset(table_scales[:].bitcast(I32), 0)
+        nc.vector.memset(w2_scales_raw[:].bitcast(I32), 0)
+        nc.vector.memset(planes[:].bitcast(I32), 0)
+        nc.vector.memset(pages[0][:], 0.0)
+
+        nc.sync.dma_start(picks[:], offs)
+        nc.sync.dma_start(places[:], offs2)
+        nc.sync.dma_start(bias2[:], b2.rearrange("(g p t) -> p g t", p=P, t=PACK))
+        nc.sync.dma_start(w2_raw[:].bitcast(I32), w2_words[0].bitcast(I32))
+        w1_rows = w1.rearrange("(p j) r -> p j r", j=PACK)
+        w1_raw0 = keep.tile([P, PACK, PASS], F32, name="w1_raw0", align_bytes=64)
+        nc.sync.dma_start(w1_raw0[:], w1_rows[:, :, 0:PASS])
+        nc.sync.dma_start(table_scales[0:P:8, :].bitcast(I32), tab_scales[0].bitcast(I32))
+        nc.sync.dma_start(w2_scales_raw[0:P:8, :].bitcast(I32), w2_scales[0].bitcast(I32))
+        nc.sync.dma_start(table[:], tab_words[0].rearrange("p t i -> p (t i)").bitcast(I32))
+        nc.gpsimd.dma_start(bias1[:], b1.rearrange("(g p t) -> p g t", p=P, t=PACK))
+        with nc.allow_non_contiguous_dma(reason="one bias value a partition"):
+            nc.gpsimd.dma_start(bias3[:], b3.rearrange("(c p) -> p c", p=P))
+
+        RAW_BYTES = PACK * PASS * 4
+        picked_scales = late.tile([P, S], U8, name="picked_scales", align_bytes=64, offset=RAW_BYTES - S // 2)
+        spread = keep.tile([P, S + H], U8, name="spread", align_bytes=64)
+        nc.vector.tensor_copy(
+            spread[:, S:].rearrange("p (g t m) -> p g t m", g=PASSES, t=PACK),
+            w2_scales_raw[:].rearrange("p (g m t) -> p g t m", g=PASSES, t=PACK),
+        )
+        nc.vector.tensor_copy(picked_scales[:], table_scales[:].indirect(picks[:]))
+        nc.vector.tensor_copy(spread[:, 0:S].bitcast(I32), picked_scales[:].bitcast(I32))
+        for q in range(4):
+            nc.sync.dma_start(
+                planes[32 * q : 32 * q + 4, :].bitcast(I32), spread[32 * q : 32 * q + 32 : 8, :].bitcast(I32)
+            )
+        v_planes = planes[:, 0:S]
+        w2_planes = planes[:, S:]
+        w1_raw1 = late.tile([P, PACK, PASS], F32, name="w1_raw1", align_bytes=64, offset=0)
+        nc.sync.dma_start(w1_raw1[:], w1_rows[:, :, PASS:])
+        w3_raw = late.tile([P, PASSES, PACK, N], F32, name="w3_raw", align_bytes=64, offset=RAW_BYTES)
+        nc.sync.dma_start(
+            w3_raw[:].rearrange("p g j n -> p g (j n)"), w3.rearrange("(g p j) n -> p g (j n)", p=P, j=PACK)
+        )
+
+        w2_codes = keep.tile([P, 2 * H], U8, name="w2_codes", align_bytes=64)
         nc.vector.tensor_copy(
             w2_codes[:].bitcast(U16).rearrange("p (g t m) -> p g t m", g=PASSES, t=PACK),
             w2_raw[:].bitcast(U16).rearrange("p (g m t) -> p g t m", g=PASSES, t=PACK),
         )
-        nc.vector.tensor_copy(picked_scales[:], table_scales[:].indirect(picks[:]))
-        nc.vector.tensor_copy(
-            w2_planes[:].rearrange("p (g t m) -> p g t m", g=PASSES, t=PACK),
-            w2_scales_raw[:].rearrange("p (g m t) -> p g t m", g=PASSES, t=PACK),
-        )
-        w1_rows = w1.rearrange("(p j) r -> p j r", j=PACK)
-        w1_raw = []
-        for g in range(PASSES):
-            raw = keep.tile([P, PACK, PASS], F32, name="w1_raw", tag="ab"[g], align_bytes=64)
-            nc.sync.dma_start(raw[:], w1_rows[:, :, g * PASS : (g + 1) * PASS])
-            w1_raw.append(raw)
-        for q in range(4):
-            nc.scalar.dma_start(
-                v_planes[32 * q : 32 * q + 4, :].bitcast(I32), picked_scales[32 * q : 32 * q + 32 : 8, :].bitcast(I32)
-            )
-        v_all = keep.tile([P, S], U32, name="v_all", tag="c", align_bytes=64)
+        v_codes = []
+        v_all = keep.tile([P, S], U32, name="v_all", tag="table_scales", align_bytes=64)
         for c in range(CHUNKS):
             nc.vector.tensor_copy(v_all[:, chunk_cols(c)], table[:].bitcast(U32).indirect(chunk_list(picks, c)))
-        v_codes = [v_all[:, chunk_cols(c)] for c in range(CHUNKS)]
-        v_scales = [v_planes[:, chunk_cols(c)] for c in range(CHUNKS)]
+            v_codes.append(v_all[:, chunk_cols(c)])
+        weights = keep.tile([P, S], F32, name="weights", tag="table", align_bytes=64)
+        nc.sync.dma_start(weights[:], wgo)
 
         w1_codes, w1_planes = [], []
         w3_codes, w3_planes = [], []
@@ -111,31 +119,22 @@ def tile_list_maxout_point_features_kernel(
             w3_codes.append(keep.tile([P, N], U32, name="w3_codes%d" % g, align_bytes=64))
             w3_planes.append(keep.tile([P, N], U8, name="w3_planes%d" % g, align_bytes=64))
 
-        def round_w1(g, copy):
-            grouped = keep.tile([P, PACK * PASS], BF16, name="w1_grouped", tag="e", align_bytes=64)
-            copy(
-                grouped[:].rearrange("p (t m j) -> p m j t", t=PACK, j=PACK),
-                w1_raw[g][:].rearrange("p j (m t) -> p m j t", t=PACK),
-            )
-            return grouped
-
-        def quantize_w1(g, grouped):
+        def prepare_w1(g, parts):
+            grouped = keep.tile([P, PACK * PASS], BF16, name="w1_grouped%d" % g, align_bytes=64)
+            dealt = grouped[:].rearrange("p (t m j) -> p m j t", t=PACK, j=PACK)
+            m0 = 0
+            for raw, copy in parts:
+                count = raw.shape[2] // PACK
+                copy(dealt[:, m0 : m0 + count], raw[:].rearrange("p j (m t) -> p m j t", t=PACK))
+                m0 = m0 + count
             nc.vector.quantize_mx(w1_codes[g][:].bitcast(FP8X4), w1_planes[g][:], grouped[:])
 
-        def load_w3(g):
-            raw = keep.tile([P, PACK, N], F32, name="w3_raw", tag="da"[g], align_bytes=64)
-            nc.sync.dma_start(raw[:], w3[g * PASS : (g + 1) * PASS, :].rearrange("(p j) n -> p j n", j=PACK))
-            return raw
-
-        def round_w3(raw, copy):
-            grouped = work.tile([P, PACK * N], BF16, name="w3_grouped", align_bytes=64)
+        def prepare_w3(g, copy):
+            grouped = keep.tile([P, PACK * N], BF16, name="w3_grouped%d" % g, align_bytes=64)
             copy(
                 grouped[:].rearrange("p (c i j) -> p c j i", i=4, j=PACK),
-                raw[:].rearrange("p j (c i) -> p c j i", i=4),
+                w3_raw[:, g].rearrange("p j (c i) -> p c j i", i=4),
             )
-            return grouped
-
-        def quantize_w3(g, grouped):
             for lo, hi in ((0, 256), (256, N)):
                 nc.vector.quantize_mx(
                     w3_codes[g][:, lo:hi].bitcast(FP8X4), w3_planes[g][:, lo:hi], grouped[:, PACK * lo : PACK * hi]
@@ -146,22 +145,22 @@ def tile_list_maxout_point_features_kernel(
         def second_pieces(c, g):
             for t in range(PACK):
                 cols = g * PASS + t * P
-                bank = psum.tile([P, CHUNK], F32, name="bank_b", tag="bank_b", bufs=2)
+                bank = psum.tile([P, CHUNK], F32, name="bank_b", tag="bank_b", bufs=3)
                 nc.tensor.matmul_mx(
                     bank[:],
                     lhsT=w2_codes[:, 2 * cols : 2 * (cols + P)].bitcast(FP4X4),
                     lhsT_scale=w2_planes[:, cols : cols + P],
                     rhs=v_codes[c].bitcast(FP8X4),
-                    rhs_scale=v_scales[c],
+                    rhs_scale=v_planes[:, chunk_cols(c)],
                     start=True,
                     stop=True,
                 )
-                piece = keep.tile([P, CHUNK], F32, name="piece", tag="piece%d%d" % (g, t), align_bytes=64)
+                piece = keep.tile([P, CHUNK], F32, name="piece", tag="piece%d%d%d" % (c, g, t), align_bytes=64)
                 nc.scalar.activation(piece[:], bank[:], IDENTITY, bias=bias2[:, g, t : t + 1])
                 second[c, g, t] = piece
 
         def maxout(c, g):
-            units = keep.tile([P, PACK, CHUNK], BF16, name="units", tag="units%d" % g, align_bytes=64)
+            units = keep.tile([P, PACK, CHUNK], BF16, name="units", tag="units%d%d" % (c, g), align_bytes=64)
             for t in range(PACK):
                 bank = psum.tile([P, CHUNK], F32, name="bank_a", tag="bank_a", bufs=3)
                 nc.tensor.matmul_mx(
@@ -169,7 +168,7 @@ def tile_list_maxout_point_features_kernel(
                     lhsT=w1_codes[g][:, t * P : (t + 1) * P].bitcast(FP8X4),
                     lhsT_scale=w1_planes[g][:, t * P : (t + 1) * P],
                     rhs=v_codes[c].bitcast(FP8X4),
-                    rhs_scale=v_scales[c],
+                    rhs_scale=v_planes[:, chunk_cols(c)],
                     start=True,
                     stop=True,
                 )
@@ -178,91 +177,71 @@ def tile_list_maxout_point_features_kernel(
                 )
             return units
 
-        def interleave(units, copy, grouped=None):
-            if grouped is None:
-                grouped = work.tile([P, PACK * CHUNK], BF16, name="h_grouped", align_bytes=64)
-            copy(
+        def interleave(units, grouped):
+            nc.scalar.copy(
                 grouped[:].rearrange("p (c i t) -> p c t i", i=4, t=PACK),
                 units[:].rearrange("p t (c i) -> p c t i", i=4),
             )
             return grouped
 
-        def quantize_h(grouped):
-            codes = work.tile([P, CHUNK], U32, name="h_codes", align_bytes=64, bufs=4)
-            planes = work.tile([P, CHUNK], U8, name="h_planes", align_bytes=64, bufs=4)
+        def quantize_h(grouped, c, g, tag):
+            codes = keep.tile([P, CHUNK], U32, name="h_codes", tag=tag, align_bytes=64)
+            planes = keep.tile([P, CHUNK], U8, name="h_planes%d%d" % (c, g), align_bytes=64)
             nc.vector.quantize_mx(codes[:].bitcast(FP8X4), planes[:], grouped[:])
             return codes, planes
 
-        def output_map(h):
-            banks = []
-            for b in range(BLOCKS):
-                bank = psum.tile([P, CHUNK], F32, name="bank_y", tag="bank_y", bufs=3)
-                for g in range(PASSES):
-                    nc.tensor.matmul_mx(
-                        bank[:],
-                        lhsT=w3_codes[g][:, b * P : (b + 1) * P].bitcast(FP8X4),
-                        lhsT_scale=w3_planes[g][:, b * P : (b + 1) * P],
-                        rhs=h[g][0][:].bitcast(FP8X4),
-                        rhs_scale=h[g][1][:],
-                        start=(g == 0),
-                        stop=(g == PASSES - 1),
-                    )
-                banks.append(bank)
-            return banks
-
-        def add_bias3(bank, b, tag):
+        def output_map(h, b, tag):
+            bank = psum.tile([P, CHUNK], F32, name="bank_y", tag="bank_y", bufs=2)
+            for g in range(PASSES):
+                nc.tensor.matmul_mx(
+                    bank[:],
+                    lhsT=w3_codes[g][:, b * P : (b + 1) * P].bitcast(FP8X4),
+                    lhsT_scale=w3_planes[g][:, b * P : (b + 1) * P],
+                    rhs=h[g][0][:].bitcast(FP8X4),
+                    rhs_scale=h[g][1][:],
+                    start=(g == 0),
+                    stop=(g == PASSES - 1),
+                )
             y = keep.tile([P, CHUNK], F32, name="y", tag=tag, align_bytes=64)
             nc.scalar.activation(y[:], bank[:], IDENTITY, bias=bias3[:, b : b + 1])
             return y
 
-        pages = []
-
         def scatter(c, b, y):
-            nc.vector.tensor_tensor(
-                pages[b][:].indirect(chunk_list(places, c)), y[:], weights[:, c * CHUNK : (c + 1) * CHUNK], MULT
-            )
+            nc.vector.tensor_tensor(pages[b][:].indirect(chunk_list(places, c)), y[:], weights[:, chunk_cols(c)], MULT)
 
-        w3_raw0 = load_w3(0)
+        PAGE_BYTES = T2 * 4
+        grouped = {}
+        for c in range(CHUNKS):
+            for g in range(PASSES):
+                if (c, g) != (0, 1):
+                    grouped[c, g] = keep.tile([P, PACK * CHUNK], BF16, name="grouped%d%d" % (c, g), align_bytes=64)
+        grouped[0, 1] = tail.tile([P, PACK * CHUNK], BF16, name="grouped01", align_bytes=64, offset=PAGE_BYTES - 2048)
+
+        prepare_w1(0, ((w1_raw0, nc.scalar.copy),))
         second_pieces(0, 0)
-        quantize_w1(0, round_w1(0, nc.vector.tensor_copy))
-        w3_raw1 = load_w3(1)
-        w1_grouped1 = round_w1(1, nc.scalar.copy)
-        weights = keep.tile([P, S], F32, name="weights", tag="b", align_bytes=64)
-        nc.sync.dma_start(weights[:], wgo)
         units00 = maxout(0, 0)
+        prepare_w1(1, ((w1_raw1, nc.vector.tensor_copy),))
         second_pieces(0, 1)
-        quantize_w1(1, w1_grouped1)
-        pages.append(keep.tile([P, T2], F32, name="page0", tag="e", align_bytes=64))
-        nc.gpsimd.memset(pages[0][:], 0.0)
-        w3_grouped0 = round_w3(w3_raw0, nc.scalar.copy)
-        grouped00 = late.tile([P, PACK * CHUNK], BF16, name="grouped00", align_bytes=64, offset=6144)
-        interleave(units00, nc.scalar.copy, grouped00)
         units01 = maxout(0, 1)
-        w3_grouped1 = round_w3(w3_raw1, nc.vector.tensor_copy)
-        grouped01 = interleave(units01, nc.vector.tensor_copy)
-        quantize_w3(0, w3_grouped0)
-        quantize_w3(1, w3_grouped1)
-        h01 = quantize_h(grouped01)
-        h00 = quantize_h(grouped00)
-        for b in (1, 2):
-            pages.append(late.tile([P, T2], F32, name="page%d" % b, align_bytes=64, offset=(b - 1) * 8192))
-            nc.gpsimd.memset(pages[b][:], 0.0)
+        interleave(units00, grouped[0, 0])
+        interleave(units01, grouped[0, 1])
         second_pieces(1, 0)
-        banks0 = output_map((h00, h01))
-        y00 = add_bias3(banks0[0], 0, "y00")
+        prepare_w3(0, nc.vector.tensor_copy)
+        prepare_w3(1, nc.vector.tensor_copy)
+        h00 = quantize_h(grouped[0, 0], 0, 0, "h_codes00")
+        h01 = quantize_h(grouped[0, 1], 0, 1, "h_codes01")
+        for b in (1, 2):
+            pages.append(tail.tile([P, T2], F32, name="page%d" % b, align_bytes=64, offset=(b - 1) * PAGE_BYTES))
+            nc.gpsimd.memset(pages[b][:], 0.0)
+        y00 = output_map((h00, h01), 0, "y00")
         units10 = maxout(1, 0)
         second_pieces(1, 1)
-        scatter(0, 0, y00)
-        grouped10 = interleave(units10, nc.scalar.copy)
         units11 = maxout(1, 1)
-        y01 = add_bias3(banks0[1], 1, "piece11")
-        grouped11 = interleave(units11, nc.scalar.copy)
-        scatter(0, 1, y01)
-        h10 = quantize_h(grouped10)
-        h11 = quantize_h(grouped11)
-        y02 = add_bias3(banks0[2], 2, "units1")
-        banks1 = output_map((h10, h11))
-        scatter(0, 2, y02)
+        scatter(0, 0, y00)
+        h10 = quantize_h(interleave(units10, grouped[1, 0]), 1, 0, "h_codes10")
+        scatter(0, 1, output_map((h00, h01), 1, "units10"))
+        h11 = quantize_h(interleave(units11, grouped[1, 1]), 1, 1, "h_codes11")
+        scatter(0, 2, output_map((h00, h01), 2, "units11"))
         for b in range(BLOCKS):
-            scatter(1, b, add_bias3(banks1[b], b, "y1%d" % b))
+            scatter(1, b, output_map((h10, h11), b, "y1%d" % b))
             nc.sync.dma_start(out[b * P : (b + 1) * P, :], pages[b][:])

@@ -35,6 +35,7 @@ def tile_list_maxout_point_features_kernel(
     with ExitStack() as ctx:
         lists = ctx.enter_context(tc.tile_pool(name="lists", bufs=1))
         keep = ctx.enter_context(tc.tile_pool(name="keep", bufs=1))
+        mid = ctx.enter_context(tc.tile_pool(name="mid", bufs=1))
         late = ctx.enter_context(tc.tile_pool(name="late", bufs=1))
         tail = ctx.enter_context(tc.tile_pool(name="tail", bufs=1))
         psum = ctx.enter_context(tc.psum_pool(name="psum", bufs=1))
@@ -112,15 +113,17 @@ def tile_list_maxout_point_features_kernel(
         nc.sync.dma_start(weights[:], wgo)
 
         w1_codes, w1_planes = [], []
-        w3_codes, w3_planes = [], []
+        w3_codes = keep.tile([P, PASSES * N], U32, name="w3_codes", align_bytes=64)
+        w3_planes = keep.tile([P, PASSES * N], U8, name="w3_planes", align_bytes=64)
         for g in range(PASSES):
             w1_codes.append(keep.tile([P, PASS], U32, name="w1_codes%d" % g, align_bytes=64))
             w1_planes.append(keep.tile([P, PASS], U8, name="w1_planes%d" % g, align_bytes=64))
-            w3_codes.append(keep.tile([P, N], U32, name="w3_codes%d" % g, align_bytes=64))
-            w3_planes.append(keep.tile([P, N], U8, name="w3_planes%d" % g, align_bytes=64))
 
         def prepare_w1(g, parts):
-            grouped = keep.tile([P, PACK * PASS], BF16, name="w1_grouped%d" % g, align_bytes=64)
+            if g == 0:
+                grouped = keep.tile([P, PACK * PASS], BF16, name="w1_grouped0", align_bytes=64)
+            else:
+                grouped = mid.tile([P, PACK * PASS], BF16, name="w1_grouped1", align_bytes=64, offset=STAGE)
             dealt = grouped[:].rearrange("p (t m j) -> p m j t", t=PACK, j=PACK)
             m0 = 0
             for raw, copy in parts:
@@ -129,15 +132,22 @@ def tile_list_maxout_point_features_kernel(
                 m0 = m0 + count
             nc.vector.quantize_mx(w1_codes[g][:].bitcast(FP8X4), w1_planes[g][:], grouped[:])
 
-        def prepare_w3(g, copy):
-            grouped = keep.tile([P, PACK * N], BF16, name="w3_grouped%d" % g, align_bytes=64)
-            copy(
-                grouped[:].rearrange("p (c i j) -> p c j i", i=4, j=PACK),
-                w3_raw[:, g].rearrange("p j (c i) -> p c j i", i=4),
+        STAGE = 3072
+        STAGE_END = STAGE + PASSES * PACK * N * 2
+
+        def prepare_w3():
+            grouped = mid.tile([P, PASSES * PACK * N], BF16, name="w3_grouped", align_bytes=64, offset=STAGE)
+            nc.gpsimd.tensor_scalar(
+                grouped[:].rearrange("p (g n j) -> p g n j", g=PASSES, j=PACK),
+                w3_raw[:].rearrange("p g j n -> p g n j"),
+                1.0,
+                0.0,
+                MULT,
+                ADD,
             )
-            for lo, hi in ((0, 256), (256, N)):
+            for lo, hi in ((0, 512), (512, PASSES * N)):
                 nc.vector.quantize_mx(
-                    w3_codes[g][:, lo:hi].bitcast(FP8X4), w3_planes[g][:, lo:hi], grouped[:, PACK * lo : PACK * hi]
+                    w3_codes[:, lo:hi].bitcast(FP8X4), w3_planes[:, lo:hi], grouped[:, PACK * lo : PACK * hi]
                 )
 
         second = {}
@@ -155,12 +165,18 @@ def tile_list_maxout_point_features_kernel(
                     start=True,
                     stop=True,
                 )
-                piece = keep.tile([P, CHUNK], F32, name="piece", tag="piece%d%d%d" % (c, g, t), align_bytes=64)
+                if (c, g, t) == (1, 1, 0):
+                    piece = mid.tile([P, CHUNK], F32, name="piece110", align_bytes=64, offset=STAGE + 1024)
+                else:
+                    piece = keep.tile([P, CHUNK], F32, name="piece", tag="piece%d%d%d" % (c, g, t), align_bytes=64)
                 nc.scalar.activation(piece[:], bank[:], IDENTITY, bias=bias2[:, g, t : t + 1])
                 second[c, g, t] = piece
 
         def maxout(c, g):
-            units = keep.tile([P, PACK, CHUNK], BF16, name="units", tag="units%d%d" % (c, g), align_bytes=64)
+            if (c, g) == (1, 1):
+                units = mid.tile([P, PACK, CHUNK], BF16, name="units11", align_bytes=64, offset=STAGE_END - 1024)
+            else:
+                units = keep.tile([P, PACK, CHUNK], BF16, name="units", tag="units%d%d" % (c, g), align_bytes=64)
             for t in range(PACK):
                 bank = psum.tile([P, CHUNK], F32, name="bank_a", tag="bank_a", bufs=3)
                 nc.tensor.matmul_mx(
@@ -185,7 +201,10 @@ def tile_list_maxout_point_features_kernel(
             return grouped
 
         def quantize_h(grouped, c, g, tag):
-            codes = keep.tile([P, CHUNK], U32, name="h_codes", tag=tag, align_bytes=64)
+            if (c, g) == (0, 0):
+                codes = mid.tile([P, CHUNK], U32, name="h_codes00", align_bytes=64, offset=STAGE + 3072)
+            else:
+                codes = keep.tile([P, CHUNK], U32, name="h_codes", tag=tag, align_bytes=64)
             planes = keep.tile([P, CHUNK], U8, name="h_planes%d%d" % (c, g), align_bytes=64)
             nc.vector.quantize_mx(codes[:].bitcast(FP8X4), planes[:], grouped[:])
             return codes, planes
@@ -195,14 +214,17 @@ def tile_list_maxout_point_features_kernel(
             for g in range(PASSES):
                 nc.tensor.matmul_mx(
                     bank[:],
-                    lhsT=w3_codes[g][:, b * P : (b + 1) * P].bitcast(FP8X4),
-                    lhsT_scale=w3_planes[g][:, b * P : (b + 1) * P],
+                    lhsT=w3_codes[:, g * N + b * P : g * N + (b + 1) * P].bitcast(FP8X4),
+                    lhsT_scale=w3_planes[:, g * N + b * P : g * N + (b + 1) * P],
                     rhs=h[g][0][:].bitcast(FP8X4),
                     rhs_scale=h[g][1][:],
                     start=(g == 0),
                     stop=(g == PASSES - 1),
                 )
-            y = keep.tile([P, CHUNK], F32, name="y", tag=tag, align_bytes=64)
+            if tag == "units11":
+                y = mid.tile([P, CHUNK], F32, name="y02", align_bytes=64, offset=STAGE_END)
+            else:
+                y = keep.tile([P, CHUNK], F32, name="y", tag=tag, align_bytes=64)
             nc.scalar.activation(y[:], bank[:], IDENTITY, bias=bias3[:, b : b + 1])
             return y
 
@@ -213,8 +235,9 @@ def tile_list_maxout_point_features_kernel(
         grouped = {}
         for c in range(CHUNKS):
             for g in range(PASSES):
-                if (c, g) != (0, 1):
+                if c == g:
                     grouped[c, g] = keep.tile([P, PACK * CHUNK], BF16, name="grouped%d%d" % (c, g), align_bytes=64)
+        grouped[1, 0] = mid.tile([P, PACK * CHUNK], BF16, name="grouped10", align_bytes=64, offset=0)
         grouped[0, 1] = tail.tile([P, PACK * CHUNK], BF16, name="grouped01", align_bytes=64, offset=PAGE_BYTES - 2048)
 
         prepare_w1(0, ((w1_raw0, nc.scalar.copy),))
@@ -224,10 +247,9 @@ def tile_list_maxout_point_features_kernel(
         second_pieces(0, 1)
         units01 = maxout(0, 1)
         interleave(units00, grouped[0, 0])
-        interleave(units01, grouped[0, 1])
         second_pieces(1, 0)
-        prepare_w3(0, nc.vector.tensor_copy)
-        prepare_w3(1, nc.vector.tensor_copy)
+        interleave(units01, grouped[0, 1])
+        prepare_w3()
         h00 = quantize_h(grouped[0, 0], 0, 0, "h_codes00")
         h01 = quantize_h(grouped[0, 1], 0, 1, "h_codes01")
         for b in (1, 2):

@@ -25,7 +25,8 @@ CHUNK = 512
 PASSES = H // PASS
 CHUNKS = S // CHUNK
 BLOCKS = N // P
-LIST_COLS = CHUNK // 16
+ROWS_AT = P - 16
+SPANS = ((0, 256), (256, 512), (512, 1024))
 
 
 def tile_list_maxout_point_features_kernel(
@@ -35,51 +36,48 @@ def tile_list_maxout_point_features_kernel(
     with ExitStack() as ctx:
         lists = ctx.enter_context(tc.tile_pool(name="lists", bufs=1))
         keep = ctx.enter_context(tc.tile_pool(name="keep", bufs=1))
-        mid = ctx.enter_context(tc.tile_pool(name="mid", bufs=1))
+        first = ctx.enter_context(tc.tile_pool(name="first", bufs=1))
+        head = ctx.enter_context(tc.tile_pool(name="head", bufs=1))
         late = ctx.enter_context(tc.tile_pool(name="late", bufs=1))
         tail = ctx.enter_context(tc.tile_pool(name="tail", bufs=1))
         psum = ctx.enter_context(tc.psum_pool(name="psum", bufs=1))
 
-        def chunk_list(tile, c):
-            return tile[:, c * LIST_COLS : (c + 1) * LIST_COLS]
-
         def chunk_cols(c):
             return slice(c * CHUNK, (c + 1) * CHUNK)
+
+        RAW_BYTES = PACK * PASS * 4
+        PAGE_BYTES = T2 * 4
 
         picks = lists.tile([P, S // 16], U16, name="picks")
         places = lists.tile([P, S // 16], U16, name="places")
         table = keep.tile([P, T], I32, name="table", tag="table", align_bytes=64)
-        table_scales = keep.tile([P, T], U8, name="table_scales", tag="table_scales", align_bytes=64)
+        table_scales = head.tile([P, T], U8, name="table_scales", align_bytes=64, offset=0)
         w2_raw = keep.tile([P, 2 * H], U8, name="w2_raw", align_bytes=64)
         w2_scales_raw = keep.tile([P, H], U8, name="w2_scales_raw", align_bytes=64)
         planes = keep.tile([P, S + H], U8, name="planes", align_bytes=64)
         bias1 = keep.tile([P, PASSES, PACK], F32, name="bias1")
         bias2 = keep.tile([P, PASSES, PACK], F32, name="bias2")
         bias3 = keep.tile([P, BLOCKS], F32, name="bias3")
-        pages = [keep.tile([P, T2], F32, name="page%d" % b, align_bytes=64) for b in range(1)]
+        pages = [keep.tile([P, T2], F32, name="page0", align_bytes=64)]
 
-        nc.gpsimd.memset(table_scales[:].bitcast(I32), 0)
-        nc.vector.memset(w2_scales_raw[:].bitcast(I32), 0)
+        nc.vector.memset(table_scales[0:ROWS_AT, :].bitcast(I32), 0)
+        nc.vector.memset(w2_scales_raw[0:ROWS_AT, :].bitcast(I32), 0)
         nc.vector.memset(planes[:].bitcast(I32), 0)
         nc.vector.memset(pages[0][:], 0.0)
 
+        nc.sync.dma_start(table_scales[ROWS_AT:P, :].bitcast(I32), tab_scales[0].bitcast(I32))
         nc.sync.dma_start(picks[:], offs)
-        nc.sync.dma_start(places[:], offs2)
-        nc.sync.dma_start(bias2[:], b2.rearrange("(g p t) -> p g t", p=P, t=PACK))
+        nc.sync.dma_start(w2_scales_raw[ROWS_AT:P, :].bitcast(I32), w2_scales[0].bitcast(I32))
         nc.sync.dma_start(w2_raw[:].bitcast(I32), w2_words[0].bitcast(I32))
-        w1_rows = w1.rearrange("(p j) r -> p j r", j=PACK)
-        w1_raw0 = keep.tile([P, PACK, PASS], F32, name="w1_raw0", align_bytes=64)
-        nc.sync.dma_start(w1_raw0[:], w1_rows[:, :, 0:PASS])
-        nc.sync.dma_start(table_scales[0:P:8, :].bitcast(I32), tab_scales[0].bitcast(I32))
-        nc.sync.dma_start(w2_scales_raw[0:P:8, :].bitcast(I32), w2_scales[0].bitcast(I32))
+        nc.sync.dma_start(bias2[:], b2.rearrange("(g p t) -> p g t", p=P, t=PACK))
+        nc.sync.dma_start(places[:], offs2)
         nc.sync.dma_start(table[:], tab_words[0].rearrange("p t i -> p (t i)").bitcast(I32))
         nc.gpsimd.dma_start(bias1[:], b1.rearrange("(g p t) -> p g t", p=P, t=PACK))
         with nc.allow_non_contiguous_dma(reason="one bias value a partition"):
             nc.gpsimd.dma_start(bias3[:], b3.rearrange("(c p) -> p c", p=P))
 
-        RAW_BYTES = PACK * PASS * 4
-        picked_scales = late.tile([P, S], U8, name="picked_scales", align_bytes=64, offset=RAW_BYTES - S // 2)
-        spread = keep.tile([P, S + H], U8, name="spread", align_bytes=64)
+        picked_scales = first.tile([P, S], U8, name="picked_scales", align_bytes=64, offset=RAW_BYTES - S // 2)
+        spread = late.tile([P, S + H], U8, name="spread", align_bytes=64, offset=RAW_BYTES - S)
         nc.vector.tensor_copy(
             spread[:, S:].rearrange("p (g t m) -> p g t m", g=PASSES, t=PACK),
             w2_scales_raw[:].rearrange("p (g m t) -> p g t m", g=PASSES, t=PACK),
@@ -88,10 +86,14 @@ def tile_list_maxout_point_features_kernel(
         nc.vector.tensor_copy(spread[:, 0:S].bitcast(I32), picked_scales[:].bitcast(I32))
         for q in range(4):
             nc.sync.dma_start(
-                planes[32 * q : 32 * q + 4, :].bitcast(I32), spread[32 * q : 32 * q + 32 : 8, :].bitcast(I32)
+                planes[32 * q : 32 * q + 4, :].bitcast(I32), spread[ROWS_AT + 4 * q : ROWS_AT + 4 * q + 4, :].bitcast(I32)
             )
         v_planes = planes[:, 0:S]
         w2_planes = planes[:, S:]
+
+        w1_rows = w1.rearrange("(p j) r -> p j r", j=PACK)
+        w1_raw0 = first.tile([P, PACK, PASS], F32, name="w1_raw0", align_bytes=64, offset=0)
+        nc.sync.dma_start(w1_raw0[:], w1_rows[:, :, 0:PASS])
         w1_raw1 = late.tile([P, PACK, PASS], F32, name="w1_raw1", align_bytes=64, offset=0)
         nc.sync.dma_start(w1_raw1[:], w1_rows[:, :, PASS:])
         w3_raw = late.tile([P, PASSES, PACK, N], F32, name="w3_raw", align_bytes=64, offset=RAW_BYTES)
@@ -104,53 +106,75 @@ def tile_list_maxout_point_features_kernel(
             w2_codes[:].bitcast(U16).rearrange("p (g t m) -> p g t m", g=PASSES, t=PACK),
             w2_raw[:].bitcast(U16).rearrange("p (g m t) -> p g t m", g=PASSES, t=PACK),
         )
+        pages.append(head.tile([P, T2], F32, name="page1", align_bytes=64, offset=0))
+        nc.vector.memset(pages[1][:], 0.0)
         v_codes = []
-        v_all = keep.tile([P, S], U32, name="v_all", tag="table_scales", align_bytes=64)
         for c in range(CHUNKS):
-            nc.vector.tensor_copy(v_all[:, chunk_cols(c)], table[:].bitcast(U32).indirect(chunk_list(picks, c)))
-            v_codes.append(v_all[:, chunk_cols(c)])
+            v_codes.append(keep.tile([P, CHUNK], U32, name="v_codes%d" % c, align_bytes=64))
+            nc.vector.tensor_copy(
+                v_codes[c][:], table[:].bitcast(U32).indirect(picks[:, c * CHUNK // 16 : (c + 1) * CHUNK // 16])
+            )
         weights = keep.tile([P, S], F32, name="weights", tag="table", align_bytes=64)
         nc.sync.dma_start(weights[:], wgo)
 
-        w1_codes, w1_planes = [], []
-        w3_codes = keep.tile([P, PASSES * N], U32, name="w3_codes", align_bytes=64)
-        w3_planes = keep.tile([P, PASSES * N], U8, name="w3_planes", align_bytes=64)
-        for g in range(PASSES):
-            w1_codes.append(keep.tile([P, PASS], U32, name="w1_codes%d" % g, align_bytes=64))
-            w1_planes.append(keep.tile([P, PASS], U8, name="w1_planes%d" % g, align_bytes=64))
+        w1_slots = {}
 
-        def prepare_w1(g, parts):
-            if g == 0:
-                grouped = keep.tile([P, PACK * PASS], BF16, name="w1_grouped0", align_bytes=64)
-            else:
-                grouped = mid.tile([P, PACK * PASS], BF16, name="w1_grouped1", align_bytes=64, offset=STAGE)
-            dealt = grouped[:].rearrange("p (t m j) -> p m j t", t=PACK, j=PACK)
-            m0 = 0
-            for raw, copy in parts:
-                count = raw.shape[2] // PACK
-                copy(dealt[:, m0 : m0 + count], raw[:].rearrange("p j (m t) -> p m j t", t=PACK))
-                m0 = m0 + count
-            nc.vector.quantize_mx(w1_codes[g][:].bitcast(FP8X4), w1_planes[g][:], grouped[:])
+        def quantize_w1(staged, g, t0, count):
+            codes = keep.tile([P, count * P], U32, name="w1_codes%d%d" % (g, t0), align_bytes=64)
+            scales = keep.tile([P, count * P], U8, name="w1_planes%d%d" % (g, t0), align_bytes=64)
+            nc.vector.quantize_mx(codes[:].bitcast(FP8X4), scales[:], staged[:])
+            for i in range(count):
+                w1_slots[g, t0 + i] = (codes[:, i * P : (i + 1) * P], scales[:, i * P : (i + 1) * P])
 
-        STAGE = 3072
-        STAGE_END = STAGE + PASSES * PACK * N * 2
+        raw0 = w1_raw0[:].rearrange("p j (m t) -> p m j t", t=PACK)
+        low = keep.tile([P, 2 * PASS], BF16, name="w1_low", align_bytes=64)
+        high = keep.tile([P, 2 * PASS], BF16, name="w1_high", tag="stage", align_bytes=64)
+        nc.vector.tensor_copy(low[:].rearrange("p (t m j) -> p m j t", t=2, j=PACK), raw0[:, :, :, 0:2])
+        nc.scalar.copy(high[:].rearrange("p (t m j) -> p m j t", t=2, j=PACK), raw0[:, :, :, 2:4])
+        quantize_w1(low, 0, 0, 2)
+        quantize_w1(high, 0, 2, 2)
 
-        def prepare_w3():
-            grouped = mid.tile([P, PASSES * PACK * N], BF16, name="w3_grouped", align_bytes=64, offset=STAGE)
+        def prepare_w1_second():
+            staged = keep.tile([P, PACK * PASS], BF16, name="w1_staged", tag="stage", align_bytes=64)
             nc.gpsimd.tensor_scalar(
-                grouped[:].rearrange("p (g n j) -> p g n j", g=PASSES, j=PACK),
-                w3_raw[:].rearrange("p g j n -> p g n j"),
+                staged[:].rearrange("p (t m j) -> p m t j", t=PACK, j=PACK),
+                w1_raw1[:].rearrange("p j (m t) -> p m t j", t=PACK),
                 1.0,
                 0.0,
                 MULT,
                 ADD,
             )
-            for lo, hi in ((0, 512), (512, PASSES * N)):
-                nc.vector.quantize_mx(
-                    w3_codes[:, lo:hi].bitcast(FP8X4), w3_planes[:, lo:hi], grouped[:, PACK * lo : PACK * hi]
+            quantize_w1(staged, 1, 0, PACK)
+
+        w3_blocks = {}
+
+        def round_w3():
+            staged = keep.tile([P, BLOCKS, PASSES, P, PACK], BF16, name="w3_staged", tag="stage", align_bytes=64)
+            for g in range(PASSES):
+                nc.gpsimd.tensor_scalar(
+                    staged[:, :, g],
+                    w3_raw[:, g].rearrange("p j (b n) -> p b n j", b=BLOCKS),
+                    1.0,
+                    0.0,
+                    MULT,
+                    ADD,
                 )
+            return staged[:].rearrange("p b g n j -> p (b g n j)")
+
+        def quantize_w3(staged, b0, count):
+            width = PASSES * P
+            codes = keep.tile([P, count * width], U32, name="w3_codes%d" % b0, align_bytes=64)
+            scales = keep.tile([P, count * width], U8, name="w3_planes%d" % b0, align_bytes=64)
+            nc.vector.quantize_mx(
+                codes[:].bitcast(FP8X4), scales[:], staged[:, PACK * b0 * width : PACK * (b0 + count) * width]
+            )
+            for i in range(count):
+                for g in range(PASSES):
+                    cols = slice(i * width + g * P, i * width + (g + 1) * P)
+                    w3_blocks[b0 + i, g] = (codes[:, cols], scales[:, cols])
 
         second = {}
+        units = {}
 
         def second_pieces(c, g):
             for t in range(PACK):
@@ -160,110 +184,103 @@ def tile_list_maxout_point_features_kernel(
                     bank[:],
                     lhsT=w2_codes[:, 2 * cols : 2 * (cols + P)].bitcast(FP4X4),
                     lhsT_scale=w2_planes[:, cols : cols + P],
-                    rhs=v_codes[c].bitcast(FP8X4),
+                    rhs=v_codes[c][:].bitcast(FP8X4),
                     rhs_scale=v_planes[:, chunk_cols(c)],
                     start=True,
                     stop=True,
                 )
-                if (c, g, t) == (1, 1, 0):
-                    piece = mid.tile([P, CHUNK], F32, name="piece110", align_bytes=64, offset=STAGE + 1024)
-                else:
-                    piece = keep.tile([P, CHUNK], F32, name="piece", tag="piece%d%d%d" % (c, g, t), align_bytes=64)
+                piece = keep.tile([P, CHUNK], F32, name="piece%d%d%d" % (c, g, t), align_bytes=64)
                 nc.scalar.activation(piece[:], bank[:], IDENTITY, bias=bias2[:, g, t : t + 1])
                 second[c, g, t] = piece
 
         def maxout(c, g):
-            if (c, g) == (1, 1):
-                units = mid.tile([P, PACK, CHUNK], BF16, name="units11", align_bytes=64, offset=STAGE_END - 1024)
-            else:
-                units = keep.tile([P, PACK, CHUNK], BF16, name="units", tag="units%d%d" % (c, g), align_bytes=64)
+            units[c, g] = keep.tile([P, PACK, CHUNK], BF16, name="units", tag="units%d%d" % (c, g), align_bytes=64)
             for t in range(PACK):
                 bank = psum.tile([P, CHUNK], F32, name="bank_a", tag="bank_a", bufs=3)
                 nc.tensor.matmul_mx(
                     bank[:],
-                    lhsT=w1_codes[g][:, t * P : (t + 1) * P].bitcast(FP8X4),
-                    lhsT_scale=w1_planes[g][:, t * P : (t + 1) * P],
-                    rhs=v_codes[c].bitcast(FP8X4),
+                    lhsT=w1_slots[g, t][0].bitcast(FP8X4),
+                    lhsT_scale=w1_slots[g, t][1],
+                    rhs=v_codes[c][:].bitcast(FP8X4),
                     rhs_scale=v_planes[:, chunk_cols(c)],
                     start=True,
                     stop=True,
                 )
                 nc.vector.scalar_tensor_tensor(
-                    units[:, t, :], bank[:], bias1[:, g, t : t + 1], second[c, g, t][:], ADD, MAX
+                    units[c, g][:, t, :], bank[:], bias1[:, g, t : t + 1], second[c, g, t][:], ADD, MAX
                 )
-            return units
 
-        def interleave(units, grouped):
+        h = {}
+
+        def quantize_h(s, g):
+            lo, hi = SPANS[s]
+            c = lo // CHUNK
+            width = hi - lo
+            if (s, g) == (1, 0):
+                grouped = tail.tile([P, PACK * width], BF16, name="grouped10", align_bytes=64, offset=0)
+            else:
+                grouped = keep.tile([P, PACK * width], BF16, name="grouped%d%d" % (s, g), align_bytes=64)
             nc.scalar.copy(
                 grouped[:].rearrange("p (c i t) -> p c t i", i=4, t=PACK),
-                units[:].rearrange("p t (c i) -> p c t i", i=4),
+                units[c, g][:, :, lo - c * CHUNK : hi - c * CHUNK].rearrange("p t (c i) -> p c t i", i=4),
             )
-            return grouped
+            codes = late.tile(
+                [P, width], U32, name="h_codes%d%d" % (s, g), align_bytes=64, offset=RAW_BYTES + 4 * (g * S + lo)
+            )
+            scales = keep.tile([P, width], U8, name="h_planes%d%d" % (s, g), align_bytes=64)
+            nc.vector.quantize_mx(codes[:].bitcast(FP8X4), scales[:], grouped[:])
+            h[s, g] = (codes, scales)
 
-        def quantize_h(grouped, c, g, tag):
-            if (c, g) == (0, 0):
-                codes = mid.tile([P, CHUNK], U32, name="h_codes00", align_bytes=64, offset=STAGE + 3072)
-            else:
-                codes = keep.tile([P, CHUNK], U32, name="h_codes", tag=tag, align_bytes=64)
-            planes = keep.tile([P, CHUNK], U8, name="h_planes%d%d" % (c, g), align_bytes=64)
-            nc.vector.quantize_mx(codes[:].bitcast(FP8X4), planes[:], grouped[:])
-            return codes, planes
-
-        def output_map(h, b, tag):
-            bank = psum.tile([P, CHUNK], F32, name="bank_y", tag="bank_y", bufs=2)
+        def place(s, b):
+            lo, hi = SPANS[s]
+            width = hi - lo
+            bank = psum.tile([P, width], F32, name="bank_y", tag="bank_y", bufs=2)
             for g in range(PASSES):
                 nc.tensor.matmul_mx(
                     bank[:],
-                    lhsT=w3_codes[:, g * N + b * P : g * N + (b + 1) * P].bitcast(FP8X4),
-                    lhsT_scale=w3_planes[:, g * N + b * P : g * N + (b + 1) * P],
-                    rhs=h[g][0][:].bitcast(FP8X4),
-                    rhs_scale=h[g][1][:],
+                    lhsT=w3_blocks[b, g][0].bitcast(FP8X4),
+                    lhsT_scale=w3_blocks[b, g][1],
+                    rhs=h[s, g][0][:].bitcast(FP8X4),
+                    rhs_scale=h[s, g][1][:],
                     start=(g == 0),
                     stop=(g == PASSES - 1),
                 )
-            if tag == "units11":
-                y = mid.tile([P, CHUNK], F32, name="y02", align_bytes=64, offset=STAGE_END)
+            if b == BLOCKS - 1 and s < 2:
+                tag = "units%d1" % s
             else:
-                y = keep.tile([P, CHUNK], F32, name="y", tag=tag, align_bytes=64)
+                tag = "y%d%d" % (s, b)
+            y = keep.tile([P, width], F32, name="y", tag=tag, align_bytes=64)
             nc.scalar.activation(y[:], bank[:], IDENTITY, bias=bias3[:, b : b + 1])
-            return y
+            nc.vector.tensor_tensor(
+                pages[b][:].indirect(places[:, lo // 16 : hi // 16]), y[:], weights[:, lo:hi], MULT
+            )
 
-        def scatter(c, b, y):
-            nc.vector.tensor_tensor(pages[b][:].indirect(chunk_list(places, c)), y[:], weights[:, chunk_cols(c)], MULT)
-
-        PAGE_BYTES = T2 * 4
-        grouped = {}
-        for c in range(CHUNKS):
-            for g in range(PASSES):
-                if c == g:
-                    grouped[c, g] = keep.tile([P, PACK * CHUNK], BF16, name="grouped%d%d" % (c, g), align_bytes=64)
-        grouped[1, 0] = mid.tile([P, PACK * CHUNK], BF16, name="grouped10", align_bytes=64, offset=0)
-        grouped[0, 1] = tail.tile([P, PACK * CHUNK], BF16, name="grouped01", align_bytes=64, offset=PAGE_BYTES - 2048)
-
-        prepare_w1(0, ((w1_raw0, nc.scalar.copy),))
         second_pieces(0, 0)
-        units00 = maxout(0, 0)
-        prepare_w1(1, ((w1_raw1, nc.vector.tensor_copy),))
-        second_pieces(0, 1)
-        units01 = maxout(0, 1)
-        interleave(units00, grouped[0, 0])
+        maxout(0, 0)
         second_pieces(1, 0)
-        interleave(units01, grouped[0, 1])
-        prepare_w3()
-        h00 = quantize_h(grouped[0, 0], 0, 0, "h_codes00")
-        h01 = quantize_h(grouped[0, 1], 0, 1, "h_codes01")
-        for b in (1, 2):
-            pages.append(tail.tile([P, T2], F32, name="page%d" % b, align_bytes=64, offset=(b - 1) * PAGE_BYTES))
-            nc.gpsimd.memset(pages[b][:], 0.0)
-        y00 = output_map((h00, h01), 0, "y00")
-        units10 = maxout(1, 0)
+        prepare_w1_second()
+        maxout(1, 0)
+        second_pieces(0, 1)
+        maxout(0, 1)
         second_pieces(1, 1)
-        units11 = maxout(1, 1)
-        scatter(0, 0, y00)
-        h10 = quantize_h(interleave(units10, grouped[1, 0]), 1, 0, "h_codes10")
-        scatter(0, 1, output_map((h00, h01), 1, "units10"))
-        h11 = quantize_h(interleave(units11, grouped[1, 1]), 1, 1, "h_codes11")
-        scatter(0, 2, output_map((h00, h01), 2, "units11"))
+        maxout(1, 1)
+        w3_staged = round_w3()
+        quantize_w3(w3_staged, 0, 1)
+        quantize_h(0, 0)
+        quantize_h(0, 1)
+        quantize_w3(w3_staged, 1, 2)
+        quantize_h(1, 0)
+        pages.append(tail.tile([P, T2], F32, name="page2", align_bytes=64, offset=0))
+        nc.gpsimd.memset(pages[2][:], 0.0)
+        place(0, 0)
+        place(0, 1)
+        quantize_h(1, 1)
+        place(0, 2)
+        quantize_h(2, 0)
+        place(1, 0)
+        place(1, 1)
+        quantize_h(2, 1)
+        place(1, 2)
         for b in range(BLOCKS):
-            scatter(1, b, output_map((h10, h11), b, "y1%d" % b))
+            place(2, b)
             nc.sync.dma_start(out[b * P : (b + 1) * P, :], pages[b][:])

@@ -37,9 +37,8 @@ def tile_list_maxout_point_features_kernel(
         lists = ctx.enter_context(tc.tile_pool(name="lists", bufs=1))
         keep = ctx.enter_context(tc.tile_pool(name="keep", bufs=1))
         first = ctx.enter_context(tc.tile_pool(name="first", bufs=1))
-        head = ctx.enter_context(tc.tile_pool(name="head", bufs=1))
+        mid = ctx.enter_context(tc.tile_pool(name="mid", bufs=1))
         late = ctx.enter_context(tc.tile_pool(name="late", bufs=1))
-        tail = ctx.enter_context(tc.tile_pool(name="tail", bufs=1))
         psum = ctx.enter_context(tc.psum_pool(name="psum", bufs=1))
 
         def chunk_cols(c):
@@ -47,12 +46,13 @@ def tile_list_maxout_point_features_kernel(
 
         RAW_BYTES = PACK * PASS * 4
         PAGE_BYTES = T2 * 4
+        STAGE_BYTES = PASSES * PACK * N * 2
 
         picks = lists.tile([P, S // 16], U16, name="picks")
         places = lists.tile([P, S // 16], U16, name="places")
         table = keep.tile([P, T], I32, name="table", tag="table", align_bytes=64)
-        table_scales = head.tile([P, T], U8, name="table_scales", align_bytes=64, offset=0)
-        w2_raw = keep.tile([P, 2 * H], U8, name="w2_raw", align_bytes=64)
+        table_scales = keep.tile([P, T], U8, name="table_scales", align_bytes=64)
+        w2_raw = first.tile([P, 2 * H], U8, name="w2_raw", align_bytes=64, offset=RAW_BYTES + PAGE_BYTES - H)
         w2_scales_raw = keep.tile([P, H], U8, name="w2_scales_raw", align_bytes=64)
         planes = keep.tile([P, S + H], U8, name="planes", align_bytes=64)
         bias1 = keep.tile([P, PASSES, PACK], F32, name="bias1")
@@ -69,9 +69,9 @@ def tile_list_maxout_point_features_kernel(
         nc.sync.dma_start(picks[:], offs)
         nc.sync.dma_start(w2_scales_raw[ROWS_AT:P, :].bitcast(I32), w2_scales[0].bitcast(I32))
         nc.sync.dma_start(w2_raw[:].bitcast(I32), w2_words[0].bitcast(I32))
-        nc.sync.dma_start(bias2[:], b2.rearrange("(g p t) -> p g t", p=P, t=PACK))
-        nc.sync.dma_start(places[:], offs2)
         nc.sync.dma_start(table[:], tab_words[0].rearrange("p t i -> p (t i)").bitcast(I32))
+        nc.sync.dma_start(places[:], offs2)
+        nc.scalar.dma_start(bias2[:], b2.rearrange("(g p t) -> p g t", p=P, t=PACK))
         nc.gpsimd.dma_start(bias1[:], b1.rearrange("(g p t) -> p g t", p=P, t=PACK))
         with nc.allow_non_contiguous_dma(reason="one bias value a partition"):
             nc.gpsimd.dma_start(bias3[:], b3.rearrange("(c p) -> p c", p=P))
@@ -106,8 +106,8 @@ def tile_list_maxout_point_features_kernel(
             w2_codes[:].bitcast(U16).rearrange("p (g t m) -> p g t m", g=PASSES, t=PACK),
             w2_raw[:].bitcast(U16).rearrange("p (g m t) -> p g t m", g=PASSES, t=PACK),
         )
-        pages.append(head.tile([P, T2], F32, name="page1", align_bytes=64, offset=0))
-        nc.vector.memset(pages[1][:], 0.0)
+        pages.append(first.tile([P, T2], F32, name="page1", align_bytes=64, offset=RAW_BYTES))
+        nc.gpsimd.memset(pages[1][:], 0.0)
         v_codes = []
         for c in range(CHUNKS):
             v_codes.append(keep.tile([P, CHUNK], U32, name="v_codes%d" % c, align_bytes=64))
@@ -128,14 +128,14 @@ def tile_list_maxout_point_features_kernel(
 
         raw0 = w1_raw0[:].rearrange("p j (m t) -> p m j t", t=PACK)
         low = keep.tile([P, 2 * PASS], BF16, name="w1_low", align_bytes=64)
-        high = keep.tile([P, 2 * PASS], BF16, name="w1_high", tag="stage", align_bytes=64)
+        high = mid.tile([P, 2 * PASS], BF16, name="w1_high", align_bytes=64, offset=0)
         nc.vector.tensor_copy(low[:].rearrange("p (t m j) -> p m j t", t=2, j=PACK), raw0[:, :, :, 0:2])
         nc.scalar.copy(high[:].rearrange("p (t m j) -> p m j t", t=2, j=PACK), raw0[:, :, :, 2:4])
         quantize_w1(low, 0, 0, 2)
         quantize_w1(high, 0, 2, 2)
 
         def prepare_w1_second():
-            staged = keep.tile([P, PACK * PASS], BF16, name="w1_staged", tag="stage", align_bytes=64)
+            staged = mid.tile([P, PACK * PASS], BF16, name="w1_staged", align_bytes=64, offset=0)
             nc.gpsimd.tensor_scalar(
                 staged[:].rearrange("p (t m j) -> p m t j", t=PACK, j=PACK),
                 w1_raw1[:].rearrange("p j (m t) -> p m t j", t=PACK),
@@ -149,7 +149,7 @@ def tile_list_maxout_point_features_kernel(
         w3_blocks = {}
 
         def round_w3():
-            staged = keep.tile([P, BLOCKS, PASSES, P, PACK], BF16, name="w3_staged", tag="stage", align_bytes=64)
+            staged = mid.tile([P, BLOCKS, PASSES, P, PACK], BF16, name="w3_staged", align_bytes=64, offset=0)
             for g in range(PASSES):
                 nc.gpsimd.tensor_scalar(
                     staged[:, :, g],
@@ -176,8 +176,8 @@ def tile_list_maxout_point_features_kernel(
         second = {}
         units = {}
 
-        def second_pieces(c, g):
-            for t in range(PACK):
+        def second_pieces(c, g, slots=range(PACK)):
+            for t in slots:
                 cols = g * PASS + t * P
                 bank = psum.tile([P, CHUNK], F32, name="bank_b", tag="bank_b", bufs=3)
                 nc.tensor.matmul_mx(
@@ -193,9 +193,12 @@ def tile_list_maxout_point_features_kernel(
                 nc.scalar.activation(piece[:], bank[:], IDENTITY, bias=bias2[:, g, t : t + 1])
                 second[c, g, t] = piece
 
-        def maxout(c, g):
-            units[c, g] = keep.tile([P, PACK, CHUNK], BF16, name="units", tag="units%d%d" % (c, g), align_bytes=64)
-            for t in range(PACK):
+        def maxout(c, g, slots=range(PACK)):
+            if (c, g) not in units:
+                units[c, g] = keep.tile(
+                    [P, PACK, CHUNK], BF16, name="units", tag="units%d%d" % (c, g), align_bytes=64
+                )
+            for t in slots:
                 bank = psum.tile([P, CHUNK], F32, name="bank_a", tag="bank_a", bufs=3)
                 nc.tensor.matmul_mx(
                     bank[:],
@@ -211,19 +214,26 @@ def tile_list_maxout_point_features_kernel(
                 )
 
         h = {}
+        woven = {}
 
-        def quantize_h(s, g):
+        def interleave(s, g):
             lo, hi = SPANS[s]
             c = lo // CHUNK
             width = hi - lo
-            if (s, g) == (1, 0):
-                grouped = tail.tile([P, PACK * width], BF16, name="grouped10", align_bytes=64, offset=0)
+            if (s, g) == (0, 1):
+                grouped = mid.tile([P, PACK * width], BF16, name="grouped01", align_bytes=64, offset=STAGE_BYTES)
             else:
                 grouped = keep.tile([P, PACK * width], BF16, name="grouped%d%d" % (s, g), align_bytes=64)
             nc.scalar.copy(
                 grouped[:].rearrange("p (c i t) -> p c t i", i=4, t=PACK),
                 units[c, g][:, :, lo - c * CHUNK : hi - c * CHUNK].rearrange("p t (c i) -> p c t i", i=4),
             )
+            woven[s, g] = grouped
+
+        def quantize_h(s, g):
+            lo, hi = SPANS[s]
+            width = hi - lo
+            grouped = woven[s, g]
             codes = late.tile(
                 [P, width], U32, name="h_codes%d%d" % (s, g), align_bytes=64, offset=RAW_BYTES + 4 * (g * S + lo)
             )
@@ -262,23 +272,31 @@ def tile_list_maxout_point_features_kernel(
         maxout(1, 0)
         second_pieces(0, 1)
         maxout(0, 1)
-        second_pieces(1, 1)
-        maxout(1, 1)
+        interleave(0, 0)
+        second_pieces(1, 1, (0, 1))
+        interleave(0, 1)
+        maxout(1, 1, (0, 1))
         w3_staged = round_w3()
         quantize_w3(w3_staged, 0, 1)
         quantize_h(0, 0)
         quantize_h(0, 1)
         quantize_w3(w3_staged, 1, 2)
-        quantize_h(1, 0)
-        pages.append(tail.tile([P, T2], F32, name="page2", align_bytes=64, offset=0))
+        pages.append(mid.tile([P, T2], F32, name="page2", align_bytes=64, offset=0))
         nc.gpsimd.memset(pages[2][:], 0.0)
+        second_pieces(1, 1, (2, 3))
+        maxout(1, 1, (2, 3))
         place(0, 0)
+        interleave(1, 0)
+        quantize_h(1, 0)
         place(0, 1)
+        interleave(1, 1)
         quantize_h(1, 1)
         place(0, 2)
+        interleave(2, 0)
         quantize_h(2, 0)
         place(1, 0)
         place(1, 1)
+        interleave(2, 1)
         quantize_h(2, 1)
         place(1, 2)
         for b in range(BLOCKS):

@@ -37,6 +37,7 @@ def tile_list_maxout_point_features_kernel(
         lists = ctx.enter_context(tc.tile_pool(name="lists", bufs=1))
         keep = ctx.enter_context(tc.tile_pool(name="keep", bufs=1))
         first = ctx.enter_context(tc.tile_pool(name="first", bufs=1))
+        head = ctx.enter_context(tc.tile_pool(name="head", bufs=1))
         mid = ctx.enter_context(tc.tile_pool(name="mid", bufs=1))
         late = ctx.enter_context(tc.tile_pool(name="late", bufs=1))
         psum = ctx.enter_context(tc.psum_pool(name="psum", bufs=1))
@@ -45,14 +46,13 @@ def tile_list_maxout_point_features_kernel(
             return slice(c * CHUNK, (c + 1) * CHUNK)
 
         RAW_BYTES = PACK * PASS * 4
-        PAGE_BYTES = T2 * 4
         STAGE_BYTES = PASSES * PACK * N * 2
 
         picks = lists.tile([P, S // 16], U16, name="picks")
         places = lists.tile([P, S // 16], U16, name="places")
         table = keep.tile([P, T], I32, name="table", tag="table", align_bytes=64)
-        table_scales = keep.tile([P, T], U8, name="table_scales", align_bytes=64)
-        w2_raw = first.tile([P, 2 * H], U8, name="w2_raw", align_bytes=64, offset=RAW_BYTES + PAGE_BYTES - H)
+        table_scales = head.tile([P, T], U8, name="table_scales", align_bytes=64, offset=0)
+        w2_raw = keep.tile([P, 2 * H], U8, name="w2_raw", align_bytes=64)
         w2_scales_raw = keep.tile([P, H], U8, name="w2_scales_raw", align_bytes=64)
         planes = keep.tile([P, S + H], U8, name="planes", align_bytes=64)
         bias1 = keep.tile([P, PASSES, PACK], F32, name="bias1")
@@ -69,9 +69,9 @@ def tile_list_maxout_point_features_kernel(
         nc.sync.dma_start(picks[:], offs)
         nc.sync.dma_start(w2_scales_raw[ROWS_AT:P, :].bitcast(I32), w2_scales[0].bitcast(I32))
         nc.sync.dma_start(w2_raw[:].bitcast(I32), w2_words[0].bitcast(I32))
+        nc.sync.dma_start(bias2[:], b2.rearrange("(g p t) -> p g t", p=P, t=PACK))
         nc.sync.dma_start(table[:], tab_words[0].rearrange("p t i -> p (t i)").bitcast(I32))
         nc.sync.dma_start(places[:], offs2)
-        nc.scalar.dma_start(bias2[:], b2.rearrange("(g p t) -> p g t", p=P, t=PACK))
         nc.gpsimd.dma_start(bias1[:], b1.rearrange("(g p t) -> p g t", p=P, t=PACK))
         with nc.allow_non_contiguous_dma(reason="one bias value a partition"):
             nc.gpsimd.dma_start(bias3[:], b3.rearrange("(c p) -> p c", p=P))
@@ -106,8 +106,8 @@ def tile_list_maxout_point_features_kernel(
             w2_codes[:].bitcast(U16).rearrange("p (g t m) -> p g t m", g=PASSES, t=PACK),
             w2_raw[:].bitcast(U16).rearrange("p (g m t) -> p g t m", g=PASSES, t=PACK),
         )
-        pages.append(first.tile([P, T2], F32, name="page1", align_bytes=64, offset=RAW_BYTES))
-        nc.gpsimd.memset(pages[1][:], 0.0)
+        pages.append(head.tile([P, T2], F32, name="page1", align_bytes=64, offset=0))
+        nc.vector.memset(pages[1][:], 0.0)
         v_codes = []
         for c in range(CHUNKS):
             v_codes.append(keep.tile([P, CHUNK], U32, name="v_codes%d" % c, align_bytes=64))
@@ -237,7 +237,8 @@ def tile_list_maxout_point_features_kernel(
             codes = late.tile(
                 [P, width], U32, name="h_codes%d%d" % (s, g), align_bytes=64, offset=RAW_BYTES + 4 * (g * S + lo)
             )
-            scales = keep.tile([P, width], U8, name="h_planes%d%d" % (s, g), align_bytes=64)
+            tag = "y01" if (s, g) == (1, 0) else "h_planes%d%d" % (s, g)
+            scales = keep.tile([P, width], U8, name="h_planes", tag=tag, align_bytes=64)
             nc.vector.quantize_mx(codes[:].bitcast(FP8X4), scales[:], grouped[:])
             h[s, g] = (codes, scales)
 
@@ -286,10 +287,10 @@ def tile_list_maxout_point_features_kernel(
         second_pieces(1, 1, (2, 3))
         maxout(1, 1, (2, 3))
         place(0, 0)
-        interleave(1, 0)
-        quantize_h(1, 0)
         place(0, 1)
+        interleave(1, 0)
         interleave(1, 1)
+        quantize_h(1, 0)
         quantize_h(1, 1)
         place(0, 2)
         interleave(2, 0)

@@ -84,10 +84,8 @@ def tile_list_maxout_point_features_kernel(
         )
         nc.vector.tensor_copy(picked_scales[:], table_scales[:].indirect(picks[:]))
         nc.vector.tensor_copy(spread[:, 0:S].bitcast(I32), picked_scales[:].bitcast(I32))
-        for q in range(4):
-            nc.sync.dma_start(
-                planes[32 * q : 32 * q + 4, :].bitcast(I32), spread[ROWS_AT + 4 * q : ROWS_AT + 4 * q + 4, :].bitcast(I32)
-            )
+        for r in range(4):
+            nc.sync.dma_start(planes[r:P:32, :].bitcast(I32), spread[ROWS_AT + r : P : 4, :].bitcast(I32))
         v_planes = planes[:, 0:S]
         w2_planes = planes[:, S:]
 
@@ -237,7 +235,7 @@ def tile_list_maxout_point_features_kernel(
             codes = late.tile(
                 [P, width], U32, name="h_codes%d%d" % (s, g), align_bytes=64, offset=RAW_BYTES + 4 * (g * S + lo)
             )
-            tag = "y01" if (s, g) == (1, 0) else "h_planes%d%d" % (s, g)
+            tag = "y00" if (s, g) == (1, 0) else "h_planes%d%d" % (s, g)
             scales = keep.tile([P, width], U8, name="h_planes", tag=tag, align_bytes=64)
             nc.vector.quantize_mx(codes[:].bitcast(FP8X4), scales[:], grouped[:])
             h[s, g] = (codes, scales)
@@ -287,10 +285,10 @@ def tile_list_maxout_point_features_kernel(
         second_pieces(1, 1, (2, 3))
         maxout(1, 1, (2, 3))
         place(0, 0)
-        place(0, 1)
         interleave(1, 0)
-        interleave(1, 1)
         quantize_h(1, 0)
+        place(0, 1)
+        interleave(1, 1)
         quantize_h(1, 1)
         place(0, 2)
         interleave(2, 0)

@@ -36,7 +36,6 @@ def tile_list_maxout_point_features_kernel(
     with ExitStack() as ctx:
         lists = ctx.enter_context(tc.tile_pool(name="lists", bufs=1))
         keep = ctx.enter_context(tc.tile_pool(name="keep", bufs=1))
-        first = ctx.enter_context(tc.tile_pool(name="first", bufs=1))
         head = ctx.enter_context(tc.tile_pool(name="head", bufs=1))
         mid = ctx.enter_context(tc.tile_pool(name="mid", bufs=1))
         late = ctx.enter_context(tc.tile_pool(name="late", bufs=1))
@@ -51,46 +50,44 @@ def tile_list_maxout_point_features_kernel(
         picks = lists.tile([P, S // 16], U16, name="picks")
         places = lists.tile([P, S // 16], U16, name="places")
         table = keep.tile([P, T], I32, name="table", tag="table", align_bytes=64)
-        table_scales = head.tile([P, T], U8, name="table_scales", align_bytes=64, offset=0)
+        table_scales = head.tile([P, T], U8, name="table_scales", align_bytes=64, offset=RAW_BYTES - T // 2)
         w2_raw = keep.tile([P, 2 * H], U8, name="w2_raw", align_bytes=64)
         w2_scales_raw = keep.tile([P, H], U8, name="w2_scales_raw", align_bytes=64)
-        planes = keep.tile([P, S + H], U8, name="planes", align_bytes=64)
+        v_planes = keep.tile([P, S], U8, name="v_planes", align_bytes=64)
+        w2_planes = keep.tile([P, H], U8, name="w2_planes", align_bytes=64)
         bias1 = keep.tile([P, PASSES, PACK], F32, name="bias1")
         bias2 = keep.tile([P, PASSES, PACK], F32, name="bias2")
         bias3 = keep.tile([P, BLOCKS], F32, name="bias3")
         pages = [keep.tile([P, T2], F32, name="page0", align_bytes=64)]
 
+        nc.vector.memset(w2_scales_raw[:].bitcast(I32), 0)
         nc.vector.memset(table_scales[0:ROWS_AT, :].bitcast(I32), 0)
-        nc.vector.memset(w2_scales_raw[0:ROWS_AT, :].bitcast(I32), 0)
-        nc.vector.memset(planes[:].bitcast(I32), 0)
+        nc.vector.memset(v_planes[:].bitcast(I32), 0)
         nc.vector.memset(pages[0][:], 0.0)
 
         nc.sync.dma_start(table_scales[ROWS_AT:P, :].bitcast(I32), tab_scales[0].bitcast(I32))
         nc.sync.dma_start(picks[:], offs)
-        nc.sync.dma_start(w2_scales_raw[ROWS_AT:P, :].bitcast(I32), w2_scales[0].bitcast(I32))
         nc.sync.dma_start(w2_raw[:].bitcast(I32), w2_words[0].bitcast(I32))
-        nc.sync.dma_start(bias2[:], b2.rearrange("(g p t) -> p g t", p=P, t=PACK))
+        for r in range(4):
+            nc.sync.dma_start(w2_scales_raw[r:P:32, :].bitcast(I32), w2_scales[0][r:16:4, :].bitcast(I32))
         nc.sync.dma_start(table[:], tab_words[0].rearrange("p t i -> p (t i)").bitcast(I32))
+        nc.sync.dma_start(bias2[:], b2.rearrange("(g p t) -> p g t", p=P, t=PACK))
         nc.sync.dma_start(places[:], offs2)
         nc.gpsimd.dma_start(bias1[:], b1.rearrange("(g p t) -> p g t", p=P, t=PACK))
         with nc.allow_non_contiguous_dma(reason="one bias value a partition"):
             nc.gpsimd.dma_start(bias3[:], b3.rearrange("(c p) -> p c", p=P))
 
-        picked_scales = first.tile([P, S], U8, name="picked_scales", align_bytes=64, offset=RAW_BYTES - S // 2)
-        spread = late.tile([P, S + H], U8, name="spread", align_bytes=64, offset=RAW_BYTES - S)
+        picked_scales = late.tile([P, S], U8, name="picked_scales", align_bytes=64, offset=RAW_BYTES - S // 2)
+        nc.vector.tensor_copy(picked_scales[:], table_scales[:].indirect(picks[:]))
+        for r in range(4):
+            nc.sync.dma_start(v_planes[r:P:32, :].bitcast(I32), picked_scales[ROWS_AT + r : P : 4, :].bitcast(I32))
         nc.vector.tensor_copy(
-            spread[:, S:].rearrange("p (g t m) -> p g t m", g=PASSES, t=PACK),
+            w2_planes[:].rearrange("p (g t m) -> p g t m", g=PASSES, t=PACK),
             w2_scales_raw[:].rearrange("p (g m t) -> p g t m", g=PASSES, t=PACK),
         )
-        nc.vector.tensor_copy(picked_scales[:], table_scales[:].indirect(picks[:]))
-        nc.vector.tensor_copy(spread[:, 0:S].bitcast(I32), picked_scales[:].bitcast(I32))
-        for r in range(4):
-            nc.sync.dma_start(planes[r:P:32, :].bitcast(I32), spread[ROWS_AT + r : P : 4, :].bitcast(I32))
-        v_planes = planes[:, 0:S]
-        w2_planes = planes[:, S:]
 
         w1_rows = w1.rearrange("(p j) r -> p j r", j=PACK)
-        w1_raw0 = first.tile([P, PACK, PASS], F32, name="w1_raw0", align_bytes=64, offset=0)
+        w1_raw0 = head.tile([P, PACK, PASS], F32, name="w1_raw0", align_bytes=64, offset=0)
         nc.sync.dma_start(w1_raw0[:], w1_rows[:, :, 0:PASS])
         w1_raw1 = late.tile([P, PACK, PASS], F32, name="w1_raw1", align_bytes=64, offset=0)
         nc.sync.dma_start(w1_raw1[:], w1_rows[:, :, PASS:])
@@ -104,7 +101,7 @@ def tile_list_maxout_point_features_kernel(
             w2_codes[:].bitcast(U16).rearrange("p (g t m) -> p g t m", g=PASSES, t=PACK),
             w2_raw[:].bitcast(U16).rearrange("p (g m t) -> p g t m", g=PASSES, t=PACK),
         )
-        pages.append(head.tile([P, T2], F32, name="page1", align_bytes=64, offset=0))
+        pages.append(head.tile([P, T2], F32, name="page1", align_bytes=64, offset=RAW_BYTES))
         nc.vector.memset(pages[1][:], 0.0)
         v_codes = []
         for c in range(CHUNKS):

@@ -49,16 +49,16 @@ def tile_list_maxout_point_features_kernel(
 
         picks = lists.tile([P, S // 16], U16, name="picks")
         places = lists.tile([P, S // 16], U16, name="places")
-        table = keep.tile([P, T], I32, name="table", tag="table", align_bytes=64)
-        table_scales = head.tile([P, T], U8, name="table_scales", align_bytes=64, offset=RAW_BYTES - T // 2)
-        w2_raw = keep.tile([P, 2 * H], U8, name="w2_raw", align_bytes=64)
-        w2_scales_raw = keep.tile([P, H], U8, name="w2_scales_raw", align_bytes=64)
-        v_planes = keep.tile([P, S], U8, name="v_planes", align_bytes=64)
-        w2_planes = keep.tile([P, H], U8, name="w2_planes", align_bytes=64)
+        table = keep.tile([P, T], I32, name="table", tag="table", align_bytes=256)
+        table_scales = head.tile([P, T], U8, name="table_scales", align_bytes=256, offset=RAW_BYTES - T // 2)
+        w2_raw = keep.tile([P, 2 * H], U8, name="w2_raw", align_bytes=256)
+        w2_scales_raw = keep.tile([P, H], U8, name="w2_scales_raw", align_bytes=256)
+        v_planes = keep.tile([P, S], U8, name="v_planes", align_bytes=256)
+        w2_planes = keep.tile([P, H], U8, name="w2_planes", align_bytes=256)
         bias1 = keep.tile([P, PASSES, PACK], F32, name="bias1")
         bias2 = keep.tile([P, PASSES, PACK], F32, name="bias2")
         bias3 = keep.tile([P, BLOCKS], F32, name="bias3")
-        pages = [keep.tile([P, T2], F32, name="page0", align_bytes=64)]
+        pages = [keep.tile([P, T2], F32, name="page0", align_bytes=256)]
 
         nc.vector.memset(w2_scales_raw[:].bitcast(I32), 0)
         nc.vector.memset(table_scales[0:ROWS_AT, :].bitcast(I32), 0)
@@ -77,7 +77,7 @@ def tile_list_maxout_point_features_kernel(
         with nc.allow_non_contiguous_dma(reason="one bias value a partition"):
             nc.gpsimd.dma_start(bias3[:], b3.rearrange("(c p) -> p c", p=P))
 
-        picked_scales = late.tile([P, S], U8, name="picked_scales", align_bytes=64, offset=RAW_BYTES - S // 2)
+        picked_scales = late.tile([P, S], U8, name="picked_scales", align_bytes=256, offset=RAW_BYTES - S // 2)
         nc.vector.tensor_copy(picked_scales[:], table_scales[:].indirect(picks[:]))
         for r in range(4):
             nc.sync.dma_start(v_planes[r:P:32, :].bitcast(I32), picked_scales[ROWS_AT + r : P : 4, :].bitcast(I32))
@@ -87,50 +87,50 @@ def tile_list_maxout_point_features_kernel(
         )
 
         w1_rows = w1.rearrange("(p j) r -> p j r", j=PACK)
-        w1_raw0 = head.tile([P, PACK, PASS], F32, name="w1_raw0", align_bytes=64, offset=0)
+        w1_raw0 = head.tile([P, PACK, PASS], F32, name="w1_raw0", align_bytes=256, offset=0)
         nc.sync.dma_start(w1_raw0[:], w1_rows[:, :, 0:PASS])
-        w1_raw1 = late.tile([P, PACK, PASS], F32, name="w1_raw1", align_bytes=64, offset=0)
+        w1_raw1 = late.tile([P, PACK, PASS], F32, name="w1_raw1", align_bytes=256, offset=0)
         nc.sync.dma_start(w1_raw1[:], w1_rows[:, :, PASS:])
-        w3_raw = late.tile([P, PASSES, PACK, N], F32, name="w3_raw", align_bytes=64, offset=RAW_BYTES)
+        w3_raw = late.tile([P, PASSES, PACK, N], F32, name="w3_raw", align_bytes=256, offset=RAW_BYTES)
         nc.sync.dma_start(
             w3_raw[:].rearrange("p g j n -> p g (j n)"), w3.rearrange("(g p j) n -> p g (j n)", p=P, j=PACK)
         )
 
-        w2_codes = keep.tile([P, 2 * H], U8, name="w2_codes", align_bytes=64)
+        w2_codes = keep.tile([P, 2 * H], U8, name="w2_codes", align_bytes=256)
         nc.vector.tensor_copy(
             w2_codes[:].bitcast(U16).rearrange("p (g t m) -> p g t m", g=PASSES, t=PACK),
             w2_raw[:].bitcast(U16).rearrange("p (g m t) -> p g t m", g=PASSES, t=PACK),
         )
-        pages.append(head.tile([P, T2], F32, name="page1", align_bytes=64, offset=RAW_BYTES))
+        pages.append(head.tile([P, T2], F32, name="page1", align_bytes=256, offset=RAW_BYTES))
         nc.vector.memset(pages[1][:], 0.0)
         v_codes = []
         for c in range(CHUNKS):
-            v_codes.append(keep.tile([P, CHUNK], U32, name="v_codes%d" % c, align_bytes=64))
+            v_codes.append(keep.tile([P, CHUNK], U32, name="v_codes%d" % c, align_bytes=256))
             nc.vector.tensor_copy(
                 v_codes[c][:], table[:].bitcast(U32).indirect(picks[:, c * CHUNK // 16 : (c + 1) * CHUNK // 16])
             )
-        weights = keep.tile([P, S], F32, name="weights", tag="table", align_bytes=64)
+        weights = keep.tile([P, S], F32, name="weights", tag="table", align_bytes=256)
         nc.sync.dma_start(weights[:], wgo)
 
         w1_slots = {}
 
         def quantize_w1(staged, g, t0, count):
-            codes = keep.tile([P, count * P], U32, name="w1_codes%d%d" % (g, t0), align_bytes=64)
-            scales = keep.tile([P, count * P], U8, name="w1_planes%d%d" % (g, t0), align_bytes=64)
+            codes = keep.tile([P, count * P], U32, name="w1_codes%d%d" % (g, t0), align_bytes=256)
+            scales = keep.tile([P, count * P], U8, name="w1_planes%d%d" % (g, t0), align_bytes=256)
             nc.vector.quantize_mx(codes[:].bitcast(FP8X4), scales[:], staged[:])
             for i in range(count):
                 w1_slots[g, t0 + i] = (codes[:, i * P : (i + 1) * P], scales[:, i * P : (i + 1) * P])
 
         raw0 = w1_raw0[:].rearrange("p j (m t) -> p m j t", t=PACK)
-        low = keep.tile([P, 2 * PASS], BF16, name="w1_low", align_bytes=64)
-        high = mid.tile([P, 2 * PASS], BF16, name="w1_high", align_bytes=64, offset=0)
+        low = keep.tile([P, 2 * PASS], BF16, name="w1_low", align_bytes=256)
+        high = mid.tile([P, 2 * PASS], BF16, name="w1_high", align_bytes=256, offset=0)
         nc.vector.tensor_copy(low[:].rearrange("p (t m j) -> p m j t", t=2, j=PACK), raw0[:, :, :, 0:2])
         nc.scalar.copy(high[:].rearrange("p (t m j) -> p m j t", t=2, j=PACK), raw0[:, :, :, 2:4])
         quantize_w1(low, 0, 0, 2)
         quantize_w1(high, 0, 2, 2)
 
         def prepare_w1_second():
-            staged = mid.tile([P, PACK * PASS], BF16, name="w1_staged", align_bytes=64, offset=0)
+            staged = mid.tile([P, PACK * PASS], BF16, name="w1_staged", align_bytes=256, offset=0)
             nc.gpsimd.tensor_scalar(
                 staged[:].rearrange("p (t m j) -> p m t j", t=PACK, j=PACK),
                 w1_raw1[:].rearrange("p j (m t) -> p m t j", t=PACK),
@@ -144,7 +144,7 @@ def tile_list_maxout_point_features_kernel(
         w3_blocks = {}
 
         def round_w3():
-            staged = mid.tile([P, BLOCKS, PASSES, P, PACK], BF16, name="w3_staged", align_bytes=64, offset=0)
+            staged = mid.tile([P, BLOCKS, PASSES, P, PACK], BF16, name="w3_staged", align_bytes=256, offset=0)
             for g in range(PASSES):
                 nc.gpsimd.tensor_scalar(
                     staged[:, :, g],
@@ -158,8 +158,8 @@ def tile_list_maxout_point_features_kernel(
 
         def quantize_w3(staged, b0, count):
             width = PASSES * P
-            codes = keep.tile([P, count * width], U32, name="w3_codes%d" % b0, align_bytes=64)
-            scales = keep.tile([P, count * width], U8, name="w3_planes%d" % b0, align_bytes=64)
+            codes = keep.tile([P, count * width], U32, name="w3_codes%d" % b0, align_bytes=256)
+            scales = keep.tile([P, count * width], U8, name="w3_planes%d" % b0, align_bytes=256)
             nc.vector.quantize_mx(
                 codes[:].bitcast(FP8X4), scales[:], staged[:, PACK * b0 * width : PACK * (b0 + count) * width]
             )
@@ -184,14 +184,14 @@ def tile_list_maxout_point_features_kernel(
                     start=True,
                     stop=True,
                 )
-                piece = keep.tile([P, CHUNK], F32, name="piece%d%d%d" % (c, g, t), align_bytes=64)
+                piece = keep.tile([P, CHUNK], F32, name="piece%d%d%d" % (c, g, t), align_bytes=256)
                 nc.scalar.activation(piece[:], bank[:], IDENTITY, bias=bias2[:, g, t : t + 1])
                 second[c, g, t] = piece
 
         def maxout(c, g, slots=range(PACK)):
             if (c, g) not in units:
                 units[c, g] = keep.tile(
-                    [P, PACK, CHUNK], BF16, name="units", tag="units%d%d" % (c, g), align_bytes=64
+                    [P, PACK, CHUNK], BF16, name="units", tag="units%d%d" % (c, g), align_bytes=256
                 )
             for t in slots:
                 bank = psum.tile([P, CHUNK], F32, name="bank_a", tag="bank_a", bufs=3)
@@ -216,9 +216,9 @@ def tile_list_maxout_point_features_kernel(
             c = lo // CHUNK
             width = hi - lo
             if (s, g) == (0, 1):
-                grouped = mid.tile([P, PACK * width], BF16, name="grouped01", align_bytes=64, offset=STAGE_BYTES)
+                grouped = mid.tile([P, PACK * width], BF16, name="grouped01", align_bytes=256, offset=STAGE_BYTES)
             else:
-                grouped = keep.tile([P, PACK * width], BF16, name="grouped%d%d" % (s, g), align_bytes=64)
+                grouped = keep.tile([P, PACK * width], BF16, name="grouped%d%d" % (s, g), align_bytes=256)
             nc.scalar.copy(
                 grouped[:].rearrange("p (c i t) -> p c t i", i=4, t=PACK),
                 units[c, g][:, :, lo - c * CHUNK : hi - c * CHUNK].rearrange("p t (c i) -> p c t i", i=4),
@@ -230,10 +230,10 @@ def tile_list_maxout_point_features_kernel(
             width = hi - lo
             grouped = woven[s, g]
             codes = late.tile(
-                [P, width], U32, name="h_codes%d%d" % (s, g), align_bytes=64, offset=RAW_BYTES + 4 * (g * S + lo)
+                [P, width], U32, name="h_codes%d%d" % (s, g), align_bytes=256, offset=RAW_BYTES + 4 * (g * S + lo)
             )
             tag = "y00" if (s, g) == (1, 0) else "h_planes%d%d" % (s, g)
-            scales = keep.tile([P, width], U8, name="h_planes", tag=tag, align_bytes=64)
+            scales = keep.tile([P, width], U8, name="h_planes", tag=tag, align_bytes=256)
             nc.vector.quantize_mx(codes[:].bitcast(FP8X4), scales[:], grouped[:])
             h[s, g] = (codes, scales)
 
@@ -255,7 +255,7 @@ def tile_list_maxout_point_features_kernel(
                 tag = "units%d1" % s
             else:
                 tag = "y%d%d" % (s, b)
-            y = keep.tile([P, width], F32, name="y", tag=tag, align_bytes=64)
+            y = keep.tile([P, width], F32, name="y", tag=tag, align_bytes=256)
             nc.scalar.activation(y[:], bank[:], IDENTITY, bias=bias3[:, b : b + 1])
             nc.vector.tensor_tensor(
                 pages[b][:].indirect(places[:, lo // 16 : hi // 16]), y[:], weights[:, lo:hi], MULT
@@ -277,7 +277,7 @@ def tile_list_maxout_point_features_kernel(
         quantize_h(0, 0)
         quantize_h(0, 1)
         quantize_w3(w3_staged, 1, 2)
-        pages.append(mid.tile([P, T2], F32, name="page2", align_bytes=64, offset=0))
+        pages.append(mid.tile([P, T2], F32, name="page2", align_bytes=256, offset=0))
         nc.gpsimd.memset(pages[2][:], 0.0)
         second_pieces(1, 1, (2, 3))
         maxout(1, 1, (2, 3))

@@ -39,6 +39,7 @@ def tile_list_maxout_point_features_kernel(
         head = ctx.enter_context(tc.tile_pool(name="head", bufs=1))
         mid = ctx.enter_context(tc.tile_pool(name="mid", bufs=1))
         late = ctx.enter_context(tc.tile_pool(name="late", bufs=1))
+        after = ctx.enter_context(tc.tile_pool(name="after", bufs=1))
         psum = ctx.enter_context(tc.psum_pool(name="psum", bufs=1))
 
         def chunk_cols(c):
@@ -52,7 +53,7 @@ def tile_list_maxout_point_features_kernel(
         table = keep.tile([P, T], I32, name="table", tag="table", align_bytes=256)
         table_scales = head.tile([P, T], U8, name="table_scales", align_bytes=256, offset=RAW_BYTES - T // 2)
         w2_raw = keep.tile([P, 2 * H], U8, name="w2_raw", align_bytes=256)
-        w2_scales_raw = keep.tile([P, H], U8, name="w2_scales_raw", align_bytes=256)
+        w2_scales_raw = after.tile([P, H], U8, name="w2_scales_raw", align_bytes=256, offset=0)
         v_planes = keep.tile([P, S], U8, name="v_planes", align_bytes=256)
         w2_planes = keep.tile([P, H], U8, name="w2_planes", align_bytes=256)
         bias1 = keep.tile([P, PASSES, PACK], F32, name="bias1")
@@ -89,7 +90,7 @@ def tile_list_maxout_point_features_kernel(
         w1_rows = w1.rearrange("(p j) r -> p j r", j=PACK)
         w1_raw0 = head.tile([P, PACK, PASS], F32, name="w1_raw0", align_bytes=256, offset=0)
         nc.sync.dma_start(w1_raw0[:], w1_rows[:, :, 0:PASS])
-        w1_raw1 = late.tile([P, PACK, PASS], F32, name="w1_raw1", align_bytes=256, offset=0)
+        w1_raw1 = after.tile([P, PACK, PASS], F32, name="w1_raw1", align_bytes=256, offset=0)
         nc.sync.dma_start(w1_raw1[:], w1_rows[:, :, PASS:])
         w3_raw = late.tile([P, PASSES, PACK, N], F32, name="w3_raw", align_bytes=256, offset=RAW_BYTES)
         nc.sync.dma_start(

@@ -56,9 +56,7 @@ def tile_list_maxout_point_features_kernel(
         w2_scales_raw = after.tile([P, H], U8, name="w2_scales_raw", align_bytes=256, offset=0)
         v_planes = keep.tile([P, S], U8, name="v_planes", align_bytes=256)
         w2_planes = keep.tile([P, H], U8, name="w2_planes", align_bytes=256)
-        bias1 = keep.tile([P, PASSES, PACK], F32, name="bias1")
         bias2 = keep.tile([P, PASSES, PACK], F32, name="bias2")
-        bias3 = keep.tile([P, BLOCKS], F32, name="bias3")
         pages = [keep.tile([P, T2], F32, name="page0", align_bytes=256)]
 
         nc.vector.memset(w2_scales_raw[:].bitcast(I32), 0)
@@ -74,9 +72,6 @@ def tile_list_maxout_point_features_kernel(
         nc.sync.dma_start(table[:], tab_words[0].rearrange("p t i -> p (t i)").bitcast(I32))
         nc.sync.dma_start(bias2[:], b2.rearrange("(g p t) -> p g t", p=P, t=PACK))
         nc.sync.dma_start(places[:], offs2)
-        nc.gpsimd.dma_start(bias1[:], b1.rearrange("(g p t) -> p g t", p=P, t=PACK))
-        with nc.allow_non_contiguous_dma(reason="one bias value a partition"):
-            nc.gpsimd.dma_start(bias3[:], b3.rearrange("(c p) -> p c", p=P))
 
         picked_scales = late.tile([P, S], U8, name="picked_scales", align_bytes=256, offset=RAW_BYTES - S // 2)
         nc.vector.tensor_copy(picked_scales[:], table_scales[:].indirect(picks[:]))
@@ -90,19 +85,24 @@ def tile_list_maxout_point_features_kernel(
         w1_rows = w1.rearrange("(p j) r -> p j r", j=PACK)
         w1_raw0 = head.tile([P, PACK, PASS], F32, name="w1_raw0", align_bytes=256, offset=0)
         nc.sync.dma_start(w1_raw0[:], w1_rows[:, :, 0:PASS])
+        bias1 = head.tile([P, PASSES, PACK], F32, name="bias1", align_bytes=256, offset=RAW_BYTES)
+        nc.sync.dma_start(bias1[:], b1.rearrange("(g p t) -> p g t", p=P, t=PACK))
         w1_raw1 = after.tile([P, PACK, PASS], F32, name="w1_raw1", align_bytes=256, offset=0)
         nc.sync.dma_start(w1_raw1[:], w1_rows[:, :, PASS:])
         w3_raw = late.tile([P, PASSES, PACK, N], F32, name="w3_raw", align_bytes=256, offset=RAW_BYTES)
         nc.sync.dma_start(
             w3_raw[:].rearrange("p g j n -> p g (j n)"), w3.rearrange("(g p j) n -> p g (j n)", p=P, j=PACK)
         )
+        bias3 = late.tile([P, BLOCKS], F32, name="bias3", align_bytes=256, offset=RAW_BYTES - 256)
+        with nc.allow_non_contiguous_dma(reason="one bias value a partition"):
+            nc.sync.dma_start(bias3[:], b3.rearrange("(c p) -> p c", p=P))
 
         w2_codes = keep.tile([P, 2 * H], U8, name="w2_codes", align_bytes=256)
         nc.vector.tensor_copy(
             w2_codes[:].bitcast(U16).rearrange("p (g t m) -> p g t m", g=PASSES, t=PACK),
             w2_raw[:].bitcast(U16).rearrange("p (g m t) -> p g t m", g=PASSES, t=PACK),
         )
-        pages.append(head.tile([P, T2], F32, name="page1", align_bytes=256, offset=RAW_BYTES))
+        pages.append(head.tile([P, T2], F32, name="page1", align_bytes=256, offset=RAW_BYTES + 256))
         nc.vector.memset(pages[1][:], 0.0)
         v_codes = []
         for c in range(CHUNKS):

@@ -40,6 +40,7 @@ def tile_list_maxout_point_features_kernel(
         mid = ctx.enter_context(tc.tile_pool(name="mid", bufs=1))
         late = ctx.enter_context(tc.tile_pool(name="late", bufs=1))
         after = ctx.enter_context(tc.tile_pool(name="after", bufs=1))
+        wide = ctx.enter_context(tc.tile_pool(name="wide", bufs=1))
         psum = ctx.enter_context(tc.psum_pool(name="psum", bufs=1))
 
         def chunk_cols(c):
@@ -50,7 +51,7 @@ def tile_list_maxout_point_features_kernel(
 
         picks = lists.tile([P, S // 16], U16, name="picks")
         places = lists.tile([P, S // 16], U16, name="places")
-        table = keep.tile([P, T], I32, name="table", tag="table", align_bytes=256)
+        table = wide.tile([P, T], I32, name="table", align_bytes=256, offset=0)
         table_scales = head.tile([P, T], U8, name="table_scales", align_bytes=256, offset=RAW_BYTES - T // 2)
         w2_raw = keep.tile([P, 2 * H], U8, name="w2_raw", align_bytes=256)
         w2_scales_raw = after.tile([P, H], U8, name="w2_scales_raw", align_bytes=256, offset=0)
@@ -93,9 +94,6 @@ def tile_list_maxout_point_features_kernel(
         nc.sync.dma_start(
             w3_raw[:].rearrange("p g j n -> p g (j n)"), w3.rearrange("(g p j) n -> p g (j n)", p=P, j=PACK)
         )
-        bias3 = late.tile([P, BLOCKS], F32, name="bias3", align_bytes=256, offset=RAW_BYTES - 256)
-        with nc.allow_non_contiguous_dma(reason="one bias value a partition"):
-            nc.sync.dma_start(bias3[:], b3.rearrange("(c p) -> p c", p=P))
 
         w2_codes = keep.tile([P, 2 * H], U8, name="w2_codes", align_bytes=256)
         nc.vector.tensor_copy(
@@ -107,11 +105,18 @@ def tile_list_maxout_point_features_kernel(
         v_codes = []
         for c in range(CHUNKS):
             v_codes.append(keep.tile([P, CHUNK], U32, name="v_codes%d" % c, align_bytes=256))
-            nc.vector.tensor_copy(
-                v_codes[c][:], table[:].bitcast(U32).indirect(picks[:, c * CHUNK // 16 : (c + 1) * CHUNK // 16])
-            )
-        weights = keep.tile([P, S], F32, name="weights", tag="table", align_bytes=256)
+            width = CHUNK // 2 if c == 0 else CHUNK
+            for lo in range(0, CHUNK, width):
+                first_entry = (c * CHUNK + lo) // 16
+                nc.vector.tensor_copy(
+                    v_codes[c][:, lo : lo + width],
+                    table[:].bitcast(U32).indirect(picks[:, first_entry : first_entry + width // 16]),
+                )
+        weights = wide.tile([P, S], F32, name="weights", align_bytes=256, offset=0)
         nc.sync.dma_start(weights[:], wgo)
+        bias3 = wide.tile([P, BLOCKS], F32, name="bias3", align_bytes=256, offset=4 * S)
+        with nc.allow_non_contiguous_dma(reason="one bias value a partition"):
+            nc.sync.dma_start(bias3[:], b3.rearrange("(c p) -> p c", p=P))
 
         w1_slots = {}
 
@@ -172,22 +177,22 @@ def tile_list_maxout_point_features_kernel(
         second = {}
         units = {}
 
-        def second_pieces(c, g, slots=range(PACK)):
+        def second_pieces(c, g, slots=range(PACK), part=slice(0, CHUNK)):
             for t in slots:
                 cols = g * PASS + t * P
-                bank = psum.tile([P, CHUNK], F32, name="bank_b", tag="bank_b", bufs=3)
+                bank = psum.tile([P, part.stop - part.start], F32, name="bank_b", tag="bank_b", bufs=3)
                 nc.tensor.matmul_mx(
                     bank[:],
                     lhsT=w2_codes[:, 2 * cols : 2 * (cols + P)].bitcast(FP4X4),
                     lhsT_scale=w2_planes[:, cols : cols + P],
-                    rhs=v_codes[c][:].bitcast(FP8X4),
-                    rhs_scale=v_planes[:, chunk_cols(c)],
+                    rhs=v_codes[c][:, part].bitcast(FP8X4),
+                    rhs_scale=v_planes[:, c * CHUNK + part.start : c * CHUNK + part.stop],
                     start=True,
                     stop=True,
                 )
-                piece = keep.tile([P, CHUNK], F32, name="piece%d%d%d" % (c, g, t), align_bytes=256)
-                nc.scalar.activation(piece[:], bank[:], IDENTITY, bias=bias2[:, g, t : t + 1])
-                second[c, g, t] = piece
+                if (c, g, t) not in second:
+                    second[c, g, t] = keep.tile([P, CHUNK], F32, name="piece%d%d%d" % (c, g, t), align_bytes=256)
+                nc.scalar.activation(second[c, g, t][:, part], bank[:], IDENTITY, bias=bias2[:, g, t : t + 1])
 
         def maxout(c, g, slots=range(PACK)):
             if (c, g) not in units:
@@ -262,8 +267,13 @@ def tile_list_maxout_point_features_kernel(
                 pages[b][:].indirect(places[:, lo // 16 : hi // 16]), y[:], weights[:, lo:hi], MULT
             )
 
-        second_pieces(0, 0)
-        maxout(0, 0)
+        halves = (slice(0, CHUNK // 2), slice(CHUNK // 2, CHUNK))
+        second_pieces(0, 0, (0, 1), halves[0])
+        second_pieces(0, 0, (0, 1), halves[1])
+        second_pieces(0, 0, (2,))
+        maxout(0, 0, (0,))
+        second_pieces(0, 0, (3,))
+        maxout(0, 0, (1, 2, 3))
         second_pieces(1, 0)
         prepare_w1_second()
         maxout(1, 0)

@@ -47,14 +47,13 @@ def tile_list_maxout_point_features_kernel(
             return slice(c * CHUNK, (c + 1) * CHUNK)
 
         RAW_BYTES = PACK * PASS * 4
-        STAGE_BYTES = PASSES * PACK * N * 2
 
         picks = lists.tile([P, S // 16], U16, name="picks")
         places = lists.tile([P, S // 16], U16, name="places")
         table = wide.tile([P, T], I32, name="table", align_bytes=256, offset=0)
         table_scales = head.tile([P, T], U8, name="table_scales", align_bytes=256, offset=RAW_BYTES - T // 2)
         w2_raw = keep.tile([P, 2 * H], U8, name="w2_raw", align_bytes=256)
-        w2_scales_raw = after.tile([P, H], U8, name="w2_scales_raw", align_bytes=256, offset=0)
+        w2_scales_raw = after.tile([P, H], U8, name="w2_scales_raw", align_bytes=256, offset=16 * (PASS // 2) - H // 2)
         v_planes = keep.tile([P, S], U8, name="v_planes", align_bytes=256)
         w2_planes = keep.tile([P, H], U8, name="w2_planes", align_bytes=256)
         bias2 = keep.tile([P, PASSES, PACK], F32, name="bias2")
@@ -88,12 +87,18 @@ def tile_list_maxout_point_features_kernel(
         nc.sync.dma_start(w1_raw0[:], w1_rows[:, :, 0:PASS])
         bias1 = head.tile([P, PASSES, PACK], F32, name="bias1", align_bytes=256, offset=RAW_BYTES)
         nc.sync.dma_start(bias1[:], b1.rearrange("(g p t) -> p g t", p=P, t=PACK))
-        w1_raw1 = after.tile([P, PACK, PASS], F32, name="w1_raw1", align_bytes=256, offset=0)
-        nc.sync.dma_start(w1_raw1[:], w1_rows[:, :, PASS:])
-        w3_raw = late.tile([P, PASSES, PACK, N], F32, name="w3_raw", align_bytes=256, offset=RAW_BYTES)
-        nc.sync.dma_start(
-            w3_raw[:].rearrange("p g j n -> p g (j n)"), w3.rearrange("(g p j) n -> p g (j n)", p=P, j=PACK)
-        )
+        HALF = PASS // 2
+        w1_raw1 = []
+        for u in range(2):
+            w1_raw1.append(after.tile([P, PACK, HALF], F32, name="w1_raw1%d" % u, align_bytes=256, offset=u * 16 * HALF))
+            nc.sync.dma_start(w1_raw1[u][:], w1_rows[:, :, PASS + u * HALF : PASS + (u + 1) * HALF])
+        w3_rows = w3.rearrange("(g p j) n -> g p (j n)", p=P, j=PACK)
+        w3_raw = []
+        for g in range(PASSES):
+            w3_raw.append(
+                late.tile([P, PACK, N], F32, name="w3_raw%d" % g, align_bytes=256, offset=RAW_BYTES + (g - 1) * 16 * N)
+            )
+            nc.sync.dma_start(w3_raw[g][:].rearrange("p j n -> p (j n)"), w3_rows[g])
 
         w2_codes = keep.tile([P, 2 * H], U8, name="w2_codes", align_bytes=256)
         nc.vector.tensor_copy(
@@ -123,44 +128,47 @@ def tile_list_maxout_point_features_kernel(
         def quantize_w1(staged, g, t0, count):
             codes = keep.tile([P, count * P], U32, name="w1_codes%d%d" % (g, t0), align_bytes=256)
             scales = keep.tile([P, count * P], U8, name="w1_planes%d%d" % (g, t0), align_bytes=256)
-            nc.vector.quantize_mx(codes[:].bitcast(FP8X4), scales[:], staged[:])
+            nc.vector.quantize_mx(codes[:].bitcast(FP8X4), scales[:], staged)
             for i in range(count):
                 w1_slots[g, t0 + i] = (codes[:, i * P : (i + 1) * P], scales[:, i * P : (i + 1) * P])
 
         raw0 = w1_raw0[:].rearrange("p j (m t) -> p m j t", t=PACK)
         low = keep.tile([P, 2 * PASS], BF16, name="w1_low", align_bytes=256)
-        high = mid.tile([P, 2 * PASS], BF16, name="w1_high", align_bytes=256, offset=0)
+        shared = keep.tile([P, PACK * CHUNK + PASSES * PACK * N], BF16, name="shared", align_bytes=256)
+        high = shared[:, PACK * CHUNK : PACK * CHUNK + 2 * PASS]
         nc.vector.tensor_copy(low[:].rearrange("p (t m j) -> p m j t", t=2, j=PACK), raw0[:, :, :, 0:2])
-        nc.scalar.copy(high[:].rearrange("p (t m j) -> p m j t", t=2, j=PACK), raw0[:, :, :, 2:4])
-        quantize_w1(low, 0, 0, 2)
+        nc.scalar.copy(high.rearrange("p (t m j) -> p m j t", t=2, j=PACK), raw0[:, :, :, 2:4])
+        quantize_w1(low[:], 0, 0, 2)
         quantize_w1(high, 0, 2, 2)
 
         def prepare_w1_second():
-            staged = mid.tile([P, PACK * PASS], BF16, name="w1_staged", align_bytes=256, offset=0)
-            nc.gpsimd.tensor_scalar(
-                staged[:].rearrange("p (t m j) -> p m t j", t=PACK, j=PACK),
-                w1_raw1[:].rearrange("p j (m t) -> p m t j", t=PACK),
-                1.0,
-                0.0,
-                MULT,
-                ADD,
-            )
-            quantize_w1(staged, 1, 0, PACK)
-
-        w3_blocks = {}
-
-        def round_w3():
-            staged = mid.tile([P, BLOCKS, PASSES, P, PACK], BF16, name="w3_staged", align_bytes=256, offset=0)
-            for g in range(PASSES):
+            staged = shared[:, 2 * CHUNK : 2 * CHUNK + PACK * PASS]
+            for u in range(2):
                 nc.gpsimd.tensor_scalar(
-                    staged[:, :, g],
-                    w3_raw[:, g].rearrange("p j (b n) -> p b n j", b=BLOCKS),
+                    staged.rearrange("p (t m j) -> p m t j", t=PACK, j=PACK)[:, u * P // 2 : (u + 1) * P // 2],
+                    w1_raw1[u][:].rearrange("p j (m t) -> p m t j", t=PACK),
                     1.0,
                     0.0,
                     MULT,
                     ADD,
                 )
-            return staged[:].rearrange("p b g n j -> p (b g n j)")
+            quantize_w1(staged, 1, 0, PACK)
+
+        w3_blocks = {}
+
+        def round_w3():
+            staged = shared[:, PACK * CHUNK :]
+            by_block = staged.rearrange("p (b g n j) -> p b g n j", b=BLOCKS, g=PASSES, j=PACK)
+            for g in range(PASSES):
+                nc.gpsimd.tensor_scalar(
+                    by_block[:, :, g],
+                    w3_raw[g][:].rearrange("p j (b n) -> p b n j", b=BLOCKS),
+                    1.0,
+                    0.0,
+                    MULT,
+                    ADD,
+                )
+            return staged
 
         def quantize_w3(staged, b0, count):
             width = PASSES * P
@@ -190,15 +198,18 @@ def tile_list_maxout_point_features_kernel(
                     start=True,
                     stop=True,
                 )
-                if (c, g, t) not in second:
+                if (c, g, t) == (1, 1, 2):
+                    second[c, g, t] = mid.tile([P, CHUNK], F32, name="piece112", align_bytes=256, offset=0)
+                elif (c, g, t) not in second:
                     second[c, g, t] = keep.tile([P, CHUNK], F32, name="piece%d%d%d" % (c, g, t), align_bytes=256)
                 nc.scalar.activation(second[c, g, t][:, part], bank[:], IDENTITY, bias=bias2[:, g, t : t + 1])
 
         def maxout(c, g, slots=range(PACK)):
-            if (c, g) not in units:
-                units[c, g] = keep.tile(
-                    [P, PACK, CHUNK], BF16, name="units", tag="units%d%d" % (c, g), align_bytes=256
-                )
+            if (c, g) == (1, 0):
+                units[c, g] = shared[:, 0 : PACK * CHUNK].rearrange("p (t j) -> p t j", t=PACK)
+            elif (c, g) not in units:
+                own = keep.tile([P, PACK, CHUNK], BF16, name="units", tag="units%d%d" % (c, g), align_bytes=256)
+                units[c, g] = own[:]
             for t in slots:
                 bank = psum.tile([P, CHUNK], F32, name="bank_a", tag="bank_a", bufs=3)
                 nc.tensor.matmul_mx(
@@ -221,10 +232,7 @@ def tile_list_maxout_point_features_kernel(
             lo, hi = SPANS[s]
             c = lo // CHUNK
             width = hi - lo
-            if (s, g) == (0, 1):
-                grouped = mid.tile([P, PACK * width], BF16, name="grouped01", align_bytes=256, offset=STAGE_BYTES)
-            else:
-                grouped = keep.tile([P, PACK * width], BF16, name="grouped%d%d" % (s, g), align_bytes=256)
+            grouped = keep.tile([P, PACK * width], BF16, name="grouped%d%d" % (s, g), align_bytes=256)
             nc.scalar.copy(
                 grouped[:].rearrange("p (c i t) -> p c t i", i=4, t=PACK),
                 units[c, g][:, :, lo - c * CHUNK : hi - c * CHUNK].rearrange("p t (c i) -> p c t i", i=4),
@@ -275,8 +283,9 @@ def tile_list_maxout_point_features_kernel(
         second_pieces(0, 0, (3,))
         maxout(0, 0, (1, 2, 3))
         second_pieces(1, 0)
+        maxout(1, 0, (0, 1))
         prepare_w1_second()
-        maxout(1, 0)
+        maxout(1, 0, (2, 3))
         second_pieces(0, 1)
         maxout(0, 1)
         interleave(0, 0)
@@ -288,10 +297,10 @@ def tile_list_maxout_point_features_kernel(
         quantize_h(0, 0)
         quantize_h(0, 1)
         quantize_w3(w3_staged, 1, 2)
-        pages.append(mid.tile([P, T2], F32, name="page2", align_bytes=256, offset=0))
-        nc.gpsimd.memset(pages[2][:], 0.0)
         second_pieces(1, 1, (2, 3))
         maxout(1, 1, (2, 3))
+        pages.append(mid.tile([P, T2], F32, name="page2", align_bytes=256, offset=0))
+        nc.gpsimd.memset(pages[2][:], 0.0)
         place(0, 0)
         interleave(1, 0)
         quantize_h(1, 0)

from contextlib import ExitStack

import concourse.mybir as mybir

K, H, N, T, S, T2 = 512, 1024, 384, 4096, 1024, 2048
FLOPS = 2 * (2 * K * H * S + H * N * S)

F32 = mybir.dt.float32
BF16 = mybir.dt.bfloat16
I32 = mybir.dt.int32
U32 = mybir.dt.uint32
U16 = mybir.dt.uint16
U8 = mybir.dt.uint8
FP8X4 = mybir.dt.float8_e4m3fn_x4
FP4X4 = mybir.dt.float4_e2m1fn_x4
ADD = mybir.AluOpType.add
MAX = mybir.AluOpType.max
MULT = mybir.AluOpType.mult
IDENTITY = mybir.ActivationFunctionType.Identity

P = 128
PACK = 4
PASS = P * PACK
CHUNK = 512
PASSES = H // PASS
CHUNKS = S // CHUNK
BLOCKS = N // P
ROWS_AT = P - 16
SPANS = ((0, 256), (256, 512), (512, 1024))


def tile_list_maxout_point_features_kernel(
    tc, tab_words, tab_scales, offs, w1, b1, w2_words, w2_scales, b2, w3, b3, wgo, offs2, out
):
    nc = tc.nc
    with ExitStack() as ctx:
        lists = ctx.enter_context(tc.tile_pool(name="lists", bufs=1))
        keep = ctx.enter_context(tc.tile_pool(name="keep", bufs=1))
        head = ctx.enter_context(tc.tile_pool(name="head", bufs=1))
        mid = ctx.enter_context(tc.tile_pool(name="mid", bufs=1))
        late = ctx.enter_context(tc.tile_pool(name="late", bufs=1))
        after = ctx.enter_context(tc.tile_pool(name="after", bufs=1))
        wide = ctx.enter_context(tc.tile_pool(name="wide", bufs=1))
        psum = ctx.enter_context(tc.psum_pool(name="psum", bufs=1))

        def chunk_cols(c):
            return slice(c * CHUNK, (c + 1) * CHUNK)

        RAW_BYTES = PACK * PASS * 4

        picks = lists.tile([P, S // 16], U16, name="picks")
        places = lists.tile([P, S // 16], U16, name="places")
        table = wide.tile([P, T], I32, name="table", align_bytes=256, offset=0)
        table_scales = head.tile([P, T], U8, name="table_scales", align_bytes=256, offset=RAW_BYTES - T // 2)
        w2_raw = keep.tile([P, 2 * H], U8, name="w2_raw", align_bytes=256)
        w2_scales_raw = after.tile([P, H], U8, name="w2_scales_raw", align_bytes=256, offset=16 * (PASS // 2) - H // 2)
        v_planes = keep.tile([P, S], U8, name="v_planes", align_bytes=256)
        w2_planes = keep.tile([P, H], U8, name="w2_planes", align_bytes=256)
        bias2 = keep.tile([P, PASSES, PACK], F32, name="bias2")
        pages = [keep.tile([P, T2], F32, name="page0", align_bytes=256)]

        nc.vector.memset(w2_scales_raw[:].bitcast(I32), 0)
        nc.vector.memset(table_scales[0:ROWS_AT, :].bitcast(I32), 0)
        nc.vector.memset(v_planes[:].bitcast(I32), 0)
        nc.vector.memset(pages[0][:], 0.0)

        nc.sync.dma_start(table_scales[ROWS_AT:P, :].bitcast(I32), tab_scales[0].bitcast(I32))
        nc.sync.dma_start(picks[:], offs)
        nc.sync.dma_start(w2_raw[:].bitcast(I32), w2_words[0].bitcast(I32))
        for r in range(4):
            nc.sync.dma_start(w2_scales_raw[r:P:32, :].bitcast(I32), w2_scales[0][r:16:4, :].bitcast(I32))
        nc.sync.dma_start(table[:], tab_words[0].rearrange("p t i -> p (t i)").bitcast(I32))
        nc.sync.dma_start(bias2[:], b2.rearrange("(g p t) -> p g t", p=P, t=PACK))
        nc.sync.dma_start(places[:], offs2)

        picked_scales = late.tile([P, S], U8, name="picked_scales", align_bytes=256, offset=RAW_BYTES - S // 2)
        nc.vector.tensor_copy(picked_scales[:], table_scales[:].indirect(picks[:]))
        for r in range(4):
            nc.sync.dma_start(v_planes[r:P:32, :].bitcast(I32), picked_scales[ROWS_AT + r : P : 4, :].bitcast(I32))
        nc.vector.tensor_copy(
            w2_planes[:].rearrange("p (g t m) -> p g t m", g=PASSES, t=PACK),
            w2_scales_raw[:].rearrange("p (g m t) -> p g t m", g=PASSES, t=PACK),
        )

        w1_rows = w1.rearrange("(p j) r -> p j r", j=PACK)
        w1_raw0 = head.tile([P, PACK, PASS], F32, name="w1_raw0", align_bytes=256, offset=0)
        nc.sync.dma_start(w1_raw0[:], w1_rows[:, :, 0:PASS])
        bias1 = head.tile([P, PASSES, PACK], F32, name="bias1", align_bytes=256, offset=RAW_BYTES)
        nc.sync.dma_start(bias1[:], b1.rearrange("(g p t) -> p g t", p=P, t=PACK))
        HALF = PASS // 2
        w1_raw1 = []
        for u in range(2):
            w1_raw1.append(after.tile([P, PACK, HALF], F32, name="w1_raw1%d" % u, align_bytes=256, offset=u * 16 * HALF))
            nc.sync.dma_start(w1_raw1[u][:], w1_rows[:, :, PASS + u * HALF : PASS + (u + 1) * HALF])
        w3_rows = w3.rearrange("(g p j) n -> g p (j n)", p=P, j=PACK)
        w3_raw = []
        for g in range(PASSES):
            w3_raw.append(
                late.tile([P, PACK, N], F32, name="w3_raw%d" % g, align_bytes=256, offset=RAW_BYTES + (g - 1) * 16 * N)
            )
            nc.sync.dma_start(w3_raw[g][:].rearrange("p j n -> p (j n)"), w3_rows[g])

        w2_codes = keep.tile([P, 2 * H], U8, name="w2_codes", align_bytes=256)
        nc.vector.tensor_copy(
            w2_codes[:].bitcast(U16).rearrange("p (g t m) -> p g t m", g=PASSES, t=PACK),
            w2_raw[:].bitcast(U16).rearrange("p (g m t) -> p g t m", g=PASSES, t=PACK),
        )
        pages.append(head.tile([P, T2], F32, name="page1", align_bytes=256, offset=RAW_BYTES + 256))
        nc.vector.memset(pages[1][:], 0.0)
        v_codes = []
        for c in range(CHUNKS):
            v_codes.append(keep.tile([P, CHUNK], U32, name="v_codes%d" % c, align_bytes=256))
            width = CHUNK // 2 if c == 0 else CHUNK
            for lo in range(0, CHUNK, width):
                first_entry = (c * CHUNK + lo) // 16
                nc.vector.tensor_copy(
                    v_codes[c][:, lo : lo + width],
                    table[:].bitcast(U32).indirect(picks[:, first_entry : first_entry + width // 16]),
                )
        weights = wide.tile([P, S], F32, name="weights", align_bytes=256, offset=0)
        nc.sync.dma_start(weights[:], wgo)
        bias3 = wide.tile([P, BLOCKS], F32, name="bias3", align_bytes=256, offset=4 * S)
        with nc.allow_non_contiguous_dma(reason="one bias value a partition"):
            nc.sync.dma_start(bias3[:], b3.rearrange("(c p) -> p c", p=P))

        w1_slots = {}

        def quantize_w1(staged, g, t0, count):
            codes = keep.tile([P, count * P], U32, name="w1_codes%d%d" % (g, t0), align_bytes=256)
            scales = keep.tile([P, count * P], U8, name="w1_planes%d%d" % (g, t0), align_bytes=256)
            nc.vector.quantize_mx(codes[:].bitcast(FP8X4), scales[:], staged)
            for i in range(count):
                w1_slots[g, t0 + i] = (codes[:, i * P : (i + 1) * P], scales[:, i * P : (i + 1) * P])

        raw0 = w1_raw0[:].rearrange("p j (m t) -> p m j t", t=PACK)
        low = keep.tile([P, 2 * PASS], BF16, name="w1_low", align_bytes=256)
        shared = keep.tile([P, PACK * CHUNK + PASSES * PACK * N], BF16, name="shared", align_bytes=256)
        high = shared[:, PACK * CHUNK : PACK * CHUNK + 2 * PASS]
        nc.vector.tensor_copy(low[:].rearrange("p (t m j) -> p m j t", t=2, j=PACK), raw0[:, :, :, 0:2])
        nc.scalar.copy(high.rearrange("p (t m j) -> p m j t", t=2, j=PACK), raw0[:, :, :, 2:4])
        quantize_w1(low[:], 0, 0, 2)
        quantize_w1(high, 0, 2, 2)

        def prepare_w1_second():
            staged = shared[:, 2 * CHUNK : 2 * CHUNK + PACK * PASS]
            for u in range(2):
                nc.gpsimd.tensor_scalar(
                    staged.rearrange("p (t m j) -> p m t j", t=PACK, j=PACK)[:, u * P // 2 : (u + 1) * P // 2],
                    w1_raw1[u][:].rearrange("p j (m t) -> p m t j", t=PACK),
                    1.0,
                    0.0,
                    MULT,
                    ADD,
                )
            quantize_w1(staged, 1, 0, PACK)

        w3_blocks = {}

        def round_w3():
            staged = shared[:, PACK * CHUNK :]
            by_block = staged.rearrange("p (b g n j) -> p b g n j", b=BLOCKS, g=PASSES, j=PACK)
            for g in range(PASSES):
                nc.gpsimd.tensor_scalar(
                    by_block[:, :, g],
                    w3_raw[g][:].rearrange("p j (b n) -> p b n j", b=BLOCKS),
                    1.0,
                    0.0,
                    MULT,
                    ADD,
                )
            return staged

        def quantize_w3(staged, b0, count):
            width = PASSES * P
            codes = keep.tile([P, count * width], U32, name="w3_codes%d" % b0, align_bytes=256)
            scales = keep.tile([P, count * width], U8, name="w3_planes%d" % b0, align_bytes=256)
            nc.vector.quantize_mx(
                codes[:].bitcast(FP8X4), scales[:], staged[:, PACK * b0 * width : PACK * (b0 + count) * width]
            )
            for i in range(count):
                for g in range(PASSES):
                    cols = slice(i * width + g * P, i * width + (g + 1) * P)
                    w3_blocks[b0 + i, g] = (codes[:, cols], scales[:, cols])

        second = {}
        units = {}

        def second_pieces(c, g, slots=range(PACK), part=slice(0, CHUNK)):
            for t in slots:
                cols = g * PASS + t * P
                bank = psum.tile([P, part.stop - part.start], F32, name="bank_b", tag="bank_b", bufs=3)
                nc.tensor.matmul_mx(
                    bank[:],
                    lhsT=w2_codes[:, 2 * cols : 2 * (cols + P)].bitcast(FP4X4),
                    lhsT_scale=w2_planes[:, cols : cols + P],
                    rhs=v_codes[c][:, part].bitcast(FP8X4),
                    rhs_scale=v_planes[:, c * CHUNK + part.start : c * CHUNK + part.stop],
                    start=True,
                    stop=True,
                )
                if (c, g, t) == (1, 1, 2):
                    second[c, g, t] = mid.tile([P, CHUNK], F32, name="piece112", align_bytes=256, offset=0)
                elif (c, g, t) not in second:
                    second[c, g, t] = keep.tile([P, CHUNK], F32, name="piece%d%d%d" % (c, g, t), align_bytes=256)
                nc.scalar.activation(second[c, g, t][:, part], bank[:], IDENTITY, bias=bias2[:, g, t : t + 1])

        def maxout(c, g, slots=range(PACK)):
            if (c, g) == (1, 0):
                units[c, g] = shared[:, 0 : PACK * CHUNK].rearrange("p (t j) -> p t j", t=PACK)
            elif (c, g) not in units:
                own = keep.tile([P, PACK, CHUNK], BF16, name="units", tag="units%d%d" % (c, g), align_bytes=256)
                units[c, g] = own[:]
            for t in slots:
                bank = psum.tile([P, CHUNK], F32, name="bank_a", tag="bank_a", bufs=3)
                nc.tensor.matmul_mx(
                    bank[:],
                    lhsT=w1_slots[g, t][0].bitcast(FP8X4),
                    lhsT_scale=w1_slots[g, t][1],
                    rhs=v_codes[c][:].bitcast(FP8X4),
                    rhs_scale=v_planes[:, chunk_cols(c)],
                    start=True,
                    stop=True,
                )
                nc.vector.scalar_tensor_tensor(
                    units[c, g][:, t, :], bank[:], bias1[:, g, t : t + 1], second[c, g, t][:], ADD, MAX
                )

        h = {}
        woven = {}

        def interleave(s, g):
            lo, hi = SPANS[s]
            c = lo // CHUNK
            width = hi - lo
            grouped = keep.tile([P, PACK * width], BF16, name="grouped%d%d" % (s, g), align_bytes=256)
            nc.scalar.copy(
                grouped[:].rearrange("p (c i t) -> p c t i", i=4, t=PACK),
                units[c, g][:, :, lo - c * CHUNK : hi - c * CHUNK].rearrange("p t (c i) -> p c t i", i=4),
            )
            woven[s, g] = grouped

        def quantize_h(s, g):
            lo, hi = SPANS[s]
            width = hi - lo
            grouped = woven[s, g]
            codes = late.tile(
                [P, width], U32, name="h_codes%d%d" % (s, g), align_bytes=256, offset=RAW_BYTES + 4 * (g * S + lo)
            )
            tag = "y00" if (s, g) == (1, 0) else "h_planes%d%d" % (s, g)
            scales = keep.tile([P, width], U8, name="h_planes", tag=tag, align_bytes=256)
            nc.vector.quantize_mx(codes[:].bitcast(FP8X4), scales[:], grouped[:])
            h[s, g] = (codes, scales)

        def place(s, b):
            lo, hi = SPANS[s]
            width = hi - lo
            bank = psum.tile([P, width], F32, name="bank_y", tag="bank_y", bufs=2)
            for g in range(PASSES):
                nc.tensor.matmul_mx(
                    bank[:],
                    lhsT=w3_blocks[b, g][0].bitcast(FP8X4),
                    lhsT_scale=w3_blocks[b, g][1],
                    rhs=h[s, g][0][:].bitcast(FP8X4),
                    rhs_scale=h[s, g][1][:],
                    start=(g == 0),
                    stop=(g == PASSES - 1),
                )
            if b == BLOCKS - 1 and s < 2:
                tag = "units%d1" % s
            else:
                tag = "y%d%d" % (s, b)
            y = keep.tile([P, width], F32, name="y", tag=tag, align_bytes=256)
            nc.scalar.activation(y[:], bank[:], IDENTITY, bias=bias3[:, b : b + 1])
            nc.vector.tensor_tensor(
                pages[b][:].indirect(places[:, lo // 16 : hi // 16]), y[:], weights[:, lo:hi], MULT
            )

        halves = (slice(0, CHUNK // 2), slice(CHUNK // 2, CHUNK))
        second_pieces(0, 0, (0, 1), halves[0])
        second_pieces(0, 0, (0, 1), halves[1])
        second_pieces(0, 0, (2,))
        maxout(0, 0, (0,))
        second_pieces(0, 0, (3,))
        maxout(0, 0, (1, 2, 3))
        second_pieces(1, 0)
        maxout(1, 0, (0, 1))
        prepare_w1_second()
        maxout(1, 0, (2, 3))
        second_pieces(0, 1)
        maxout(0, 1)
        interleave(0, 0)
        second_pieces(1, 1, (0, 1))
        interleave(0, 1)
        maxout(1, 1, (0, 1))
        w3_staged = round_w3()
        quantize_w3(w3_staged, 0, 1)
        quantize_h(0, 0)
        quantize_h(0, 1)
        quantize_w3(w3_staged, 1, 2)
        second_pieces(1, 1, (2, 3))
        maxout(1, 1, (2, 3))
        pages.append(mid.tile([P, T2], F32, name="page2", align_bytes=256, offset=0))
        nc.gpsimd.memset(pages[2][:], 0.0)
        place(0, 0)
        interleave(1, 0)
        quantize_h(1, 0)
        place(0, 1)
        interleave(1, 1)
        quantize_h(1, 1)
        place(0, 2)
        interleave(2, 0)
        quantize_h(2, 0)
        place(1, 0)
        place(1, 1)
        interleave(2, 1)
        quantize_h(2, 1)
        place(1, 2)
        for b in range(BLOCKS):
            place(2, b)
            nc.sync.dma_start(out[b * P : (b + 1) * P, :], pages[b][:])
